import numpy as np
import ml_dtypes


def mxq(x, axis, fmt="e4m3"):
    dtype, down = {"e4m3": (ml_dtypes.float8_e4m3fn, 7), "e5m2": (ml_dtypes.float8_e5m2, 14)}[fmt]
    v = np.moveaxis(np.asarray(x, np.float32).astype(ml_dtypes.bfloat16).astype(np.float64), axis, -1)
    blocks = v.reshape(v.shape[:-1] + (-1, 32))
    amax = np.abs(blocks).max(-1, keepdims=True)
    byte = np.maximum(np.where(amax > 0, np.frexp(amax)[1] - 1 + 127, 0) - down, 1)
    scale = np.exp2(byte - 127.0)
    codes = (blocks / scale).astype(np.float32).astype(dtype).astype(np.float64)
    return np.moveaxis((codes * scale).reshape(v.shape), -1, axis)


WIDE = False


def mx_kscale(k):
    if not WIDE:
        return np.ones(k)
    levels = np.array([10, -10, 5, -5, 0])
    if k % 512:
        return np.exp2(np.random.permutation(np.resize(levels, k // 32))).repeat(32)
    a = np.empty((k // 512, 16))
    for p in range(k // 512):
        a[p, :8] = np.random.permutation(np.resize(levels, 8))
        for g in range(8):
            far = levels[np.abs(levels - a[p, g]) >= 10]
            a[p, g + 8] = far[np.random.randint(len(far))]
    return np.exp2(a.ravel()).repeat(32)


def f64(x):
    return np.asarray(x).astype(np.float64)


def striped(idx):
    return np.tile(idx.reshape(-1, 16).T, (8, 1)).astype(np.uint16)


def unstriped(offs):
    return offs[:16].T.reshape(-1).astype(np.int64)


E2M1 = np.array([0.0, 0.5, 1.0, 1.5, 2.0, 3.0, 4.0, 6.0, -0.0, -0.5, -1.0, -1.5, -2.0, -3.0, -4.0, -6.0])


def pack_weight(w, fmt):
    k, n = w.shape
    w = f64(np.asarray(w, np.float32).astype(ml_dtypes.bfloat16)).reshape(k // 32, 32, n)
    amax = np.abs(w).max(1)
    if fmt == "e4m3":
        byte = np.frexp(amax)[1] - 1 + 127 - 7
    else:
        mant, ex = np.frexp(amax / 6.0)
        byte = np.where(mant > 0.5, ex, ex - 1) + 127
    byte = np.clip(np.where(amax > 0, byte, 1), 1, 254)
    scaled = (w * np.exp2(127.0 - byte)[:, None, :]).reshape(k, n).astype(np.float32)
    by_word = np.ascontiguousarray(scaled.reshape(k // 512, 128, 4, n).transpose(0, 1, 3, 2))
    if fmt == "e4m3":
        words = by_word.astype(ml_dtypes.float8_e4m3fn).view(np.uint8)
    else:
        c = by_word.astype(ml_dtypes.float4_e2m1fn).view(np.uint8) & 0xF
        words = (c[..., 0::2] | (c[..., 1::2] << 4)).reshape(k // 512, 128, 2 * n)
    return np.ascontiguousarray(words), np.ascontiguousarray(byte.astype(np.uint8).reshape(k // 512, 16, n))


def unpack_weight(words, scales, fmt):
    g, _, n = scales.shape
    words = np.ascontiguousarray(words).reshape(g, 128, n, -1)
    if fmt == "e4m3":
        vals = words.view(ml_dtypes.float8_e4m3fn).astype(np.float64)
    else:
        nib = np.empty((g, 128, n, 4), np.uint8)
        nib[..., 0::2] = words & 0xF
        nib[..., 1::2] = words >> 4
        vals = E2M1[nib]
    vals = vals * np.repeat(np.exp2(scales.astype(np.float64) - 127.0), 8, axis=1)[..., None]
    return vals.transpose(0, 1, 3, 2).reshape(g * 512, n)


def gelu(v):
    return 0.5 * v * (1.0 + np.tanh(np.sqrt(2.0 / np.pi) * (v + 0.044715 * v**3)))


K, H, N, T, S, T2, P = 1024, 1024, 512, 4096, 1024, 2048, 1024

def setup_inputs():
    n = np.random.standard_normal
    s = mx_kscale(K)[:, None]
    u = mx_kscale(H)[:, None]
    tab_words, tab_scales = pack_weight(n((K, T)) * s, "e4m3")
    w2_words, w2_scales = pack_weight(n((K, H)) / np.sqrt(K) * u.T / s, "e2m1")
    return {
        "tab_words": tab_words, "tab_scales": tab_scales,
        "offs": striped(np.random.permutation(T)[:S]),
        "w1": (n((K, H)) / np.sqrt(K) * u.T / s).astype(np.float32),
        "w2_words": w2_words, "w2_scales": w2_scales,
        "page0": (n((H, T2)) * u).astype(np.float32),
        "wgs": np.exp(0.3 * n((128, S))).astype(np.float32),
        "offs2": striped(np.random.permutation(T2)[:S]),
        "offs3": striped(np.random.permutation(T2)[:P]),
        "offs4": striped(np.random.permutation(T2)[:P]),
        "gain": (np.random.uniform(0.5, 2.0, H) / u[:, 0]).astype(np.float32),
        "w3": (n((H, N)) / np.sqrt(H) / u).astype(np.float32),
        "rel": np.random.uniform(0.5, 2.0, N).astype(np.float32),
    }

def reference(tab_words, tab_scales, offs, w1, w2_words, w2_scales, page0, wgs,
              offs2, offs3, offs4, gain, w3, rel):
    v = unpack_weight(tab_words, tab_scales, "e4m3")[:, unstriped(offs)]
    w2 = unpack_weight(w2_words, w2_scales, "e2m1")
    h1 = mxq(f64(w1), 0, "e4m3").T @ v
    h2 = w2.T @ v
    h = np.maximum(h1, h2)
    page = f64(page0).copy()
    page[:, unstriped(offs2)] = np.tile(f64(wgs), (H // 128, 1)) * h
    x1 = page[:, unstriped(offs3)]
    x2 = page[:, unstriped(offs4)]
    z = x2 * x1 * f64(gain)[:, None]
    y = mxq(f64(w3), 0, "e4m3").T @ mxq(z, 0, "e4m3")
    return y * f64(rel)[:, None]

@@ -1,0 +1,319 @@
+from contextlib import ExitStack
+
+import concourse.mybir as mybir
+
+K, H, N, T, S, T2, M = 1024, 1024, 512, 4096, 1024, 2048, 1024
+FLOPS = 2 * (2 * K * H * S + H * N * M)
+
+F32 = mybir.dt.float32
+BF16 = mybir.dt.bfloat16
+I32 = mybir.dt.int32
+U32 = mybir.dt.uint32
+U16 = mybir.dt.uint16
+U8 = mybir.dt.uint8
+FP8X4 = mybir.dt.float8_e4m3fn_x4
+FP4X4 = mybir.dt.float4_e2m1fn_x4
+MULT = mybir.AluOpType.mult
+MAX = mybir.AluOpType.max
+COPY = mybir.ActivationFunctionType.Copy
+
+P = 128
+PACK = 4
+K_PASS = P * PACK
+BANK = 512
+TILES = H // P
+TAIL_CHUNKS = ((0, 512), (512, 768), (768, 1024))
+
+
+def tile_list_royal_succession_features_kernel(
+    tc, tab_words, tab_scales, offs, w1, w2_words, w2_scales, page0, wgs, offs2, offs3, offs4, gain, w3, rel, out
+):
+    nc = tc.nc
+    with ExitStack() as ctx:
+        held = ctx.enter_context(tc.tile_pool(name="held", bufs=1))
+        big = ctx.enter_context(tc.tile_pool(name="big", bufs=2))
+        pages = ctx.enter_context(tc.tile_pool(name="pages", bufs=5))
+        stage = ctx.enter_context(tc.tile_pool(name="stage", bufs=3))
+        work = ctx.enter_context(tc.tile_pool(name="work", bufs=2))
+        psum = ctx.enter_context(tc.psum_pool(name="psum", bufs=8))
+
+        def load_list(name, src):
+            t = held.tile([P, S // 16], U16, name=name)
+            nc.sync.dma_start(t[:], src)
+            return t
+
+        def cols(lst, lo, hi):
+            return lst[:, lo // 16 : hi // 16]
+
+        scale_rows = held.tile([P, T], U8, align_bytes=64)
+        nc.vector.memset(scale_rows[32:64, :].bitcast(I32), 0)
+        nc.vector.memset(scale_rows[64:128, :].bitcast(I32), 0)
+        w2s = held.tile([P, 2, H], U8, align_bytes=64)
+        nc.gpsimd.memset(w2s[:].rearrange("p a c -> p (a c)").bitcast(I32), 0)
+        v_scales = held.tile([P, 2, S], U8, align_bytes=64)
+        nc.vector.memset(v_scales[:].rearrange("p a c -> p (a c)").bitcast(I32), 0)
+        for q in range(4):
+            nc.gpsimd.dma_start(
+                w2s[32 * q : 32 * q + 4, :, :].bitcast(I32),
+                w2_scales[:, 4 * q : 4 * q + 4, :].rearrange("a r c -> r a c").bitcast(I32),
+            )
+
+        list1 = load_list("list1", offs)
+        nc.sync.dma_start(scale_rows[0:32, :].bitcast(I32), tab_scales.rearrange("a q t -> q a t").bitcast(I32))
+
+        def load_table(a):
+            t = big.tile([P, T], U32, name="big", align_bytes=64)
+            nc.sync.dma_start(t[:].bitcast(I32), tab_words[a].rearrange("p t i -> p (t i)").bitcast(I32))
+            return t
+
+        tab0 = load_table(0)
+        w2w = held.tile([P, 2, 2 * H], U8, align_bytes=64)
+        nc.sync.dma_start(w2w[:].bitcast(I32), w2_words.rearrange("a p c -> p a c").bitcast(I32))
+
+        def load_w1_natural(c):
+            raw = stage.tile([P, 2, PACK, P], F32, name="raw")
+            for a in range(2):
+                rows = w1[K_PASS * a : K_PASS * (a + 1), P * c : P * (c + 1)]
+                nc.sync.dma_start(raw[:, a, :, :], rows.rearrange("(p j) c -> p j c", j=PACK))
+            grouped = stage.tile([P, 2, P, PACK], BF16, name="grouped", align_bytes=64)
+            for a in range(2):
+                nc.scalar.copy(
+                    grouped[:, a, :, :].rearrange("p (c i) j -> p c j i", i=4),
+                    raw[:, a, :, :].rearrange("p j (c i) -> p c j i", i=4),
+                )
+            return grouped[:].rearrange("p a c j -> p (a c j)")
+
+        def load_rows(src, permuted):
+            raw = stage.tile([P, PACK, BANK], F32, name="raw")
+            nc.sync.dma_start(raw[:], src.rearrange("(p j) c -> p j c", j=PACK))
+            grouped = stage.tile([P, BANK, PACK], BF16, name="grouped", align_bytes=64)
+            if permuted:
+                nc.scalar.copy(
+                    grouped[:].rearrange("p (t m) j -> p t m j", t=PACK),
+                    raw[:].rearrange("p j (m t) -> p t m j", t=PACK),
+                )
+            else:
+                nc.scalar.copy(
+                    grouped[:].rearrange("p (c i) j -> p c j i", i=4),
+                    raw[:].rearrange("p j (c i) -> p c j i", i=4),
+                )
+            return grouped[:].rearrange("p c j -> p (c j)")
+
+        def quantize(codes, scales, grouped):
+            nc.vector.quantize_mx(out=codes.bitcast(FP8X4), scales=scales, in_=grouped)
+
+        def load_page(i):
+            t = pages.tile([P, T2], F32, name="page")
+            if i < 4:
+                src = page0[P * i : P * (i + 1), :]
+            else:
+                src = page0[K_PASS:, :].rearrange("(p t) c -> t p c", t=PACK)[i - 4]
+            nc.sync.dma_start(t[:], src)
+            return t
+
+        w1_grouped = {0: load_w1_natural(0)}
+        tab1 = load_table(1)
+        list2 = load_list("list2", offs2)
+        wgs_nat = held.tile([P, S], F32)
+        nc.sync.dma_start(wgs_nat[:], wgs)
+        page = {0: load_page(0)}
+
+        picked_scales = held.tile([P, S], U8, align_bytes=64)
+        nc.vector.tensor_copy(picked_scales[:], scale_rows[:].indirect(list1[:]))
+        for q in range(4):
+            nc.scalar.dma_start(
+                v_scales[32 * q : 32 * q + 4, :, :].bitcast(I32), picked_scales[8 * q : 8 * q + 8, :].bitcast(I32)
+            )
+        v_words = [held.tile([P, S], U32, name="v_words%d" % a, align_bytes=64) for a in range(2)]
+        nc.vector.tensor_copy(v_words[0][:], tab0[:].indirect(list1[:]))
+
+        w2w_perm = held.tile([P, 2, H], U8, align_bytes=64)
+        nc.vector.tensor_copy(
+            w2w_perm[:].bitcast(U16).rearrange("p a (t m) -> p a t m", t=PACK),
+            w2w[:, :, H:].bitcast(U16).rearrange("p a (m t) -> p a t m", t=PACK),
+        )
+        w2s_perm = held.tile([P, 2, K_PASS], U8, align_bytes=64)
+        nc.vector.tensor_copy(
+            w2s_perm[:].rearrange("p a (t m) -> p a t m", t=PACK),
+            w2s[:, :, K_PASS:].rearrange("p a (m t) -> p a t m", t=PACK),
+        )
+
+        w1c_nat = [held.tile([P, 2 * P], U32, name="w1c%d" % c, align_bytes=64) for c in range(4)]
+        w1s_nat = [held.tile([P, 2 * P], U8, name="w1s%d" % c, align_bytes=64) for c in range(4)]
+        w1c_perm = [held.tile([P, K_PASS], U32, name="w1cp%d" % a, align_bytes=64) for a in range(2)]
+        w1s_perm = [held.tile([P, K_PASS], U8, name="w1sp%d" % a, align_bytes=64) for a in range(2)]
+        w3c = [held.tile([P, N], U32, name="w3c%d" % b, align_bytes=64) for b in range(2)]
+        w3s = [held.tile([P, N], U8, name="w3s%d" % b, align_bytes=64) for b in range(2)]
+        zc = [held.tile([P, M], U32, name="zc%d" % b, align_bytes=64) for b in range(2)]
+        zs = [held.tile([P, M], U8, name="zs%d" % b, align_bytes=64) for b in range(2)]
+
+        quantize(w1c_nat[0][:], w1s_nat[0][:], w1_grouped[0])
+        for half in range(2):
+            lo, hi = BANK * half, BANK * (half + 1)
+            nc.vector.tensor_copy(v_words[1][:, lo:hi], tab1[:].indirect(cols(list1, lo, hi)))
+
+        def stationary(i, a):
+            if i < 4:
+                c1 = slice(P * a, P * (a + 1))
+                return (
+                    w1c_nat[i][:, c1].bitcast(FP8X4),
+                    w1s_nat[i][:, c1],
+                    w2w[:, a, 2 * P * i : 2 * P * (i + 1)].bitcast(FP4X4),
+                    w2s[:, a, P * i : P * (i + 1)],
+                )
+            t = i - 4
+            c1 = slice(P * t, P * (t + 1))
+            return (
+                w1c_perm[a][:, c1].bitcast(FP8X4),
+                w1s_perm[a][:, c1],
+                w2w_perm[:, a, 2 * P * t : 2 * P * (t + 1)].bitcast(FP4X4),
+                w2s_perm[:, a, c1],
+            )
+
+        h = {}
+
+        def first_stage(i, half):
+            if half == 0:
+                h[i] = work.tile([P, S], F32, name="h")
+            c = slice(BANK * half, BANK * (half + 1))
+            h1 = psum.tile([P, BANK], F32, name="bank")
+            h2 = psum.tile([P, BANK], F32, name="bank")
+            for a in range(2):
+                c1, s1, c2, s2 = stationary(i, a)
+                moving = v_words[a][:, c].bitcast(FP8X4)
+                for acc, codes, scales in ((h1, c1, s1), (h2, c2, s2)):
+                    nc.tensor.matmul_mx(
+                        out=acc[:], lhsT=codes, lhsT_scale=scales, rhs=moving, rhs_scale=v_scales[:, a, c],
+                        start=(a == 0), stop=(a == 1),
+                    )
+            h1_sb = stage.tile([P, BANK], F32, name="h1_sb")
+            nc.scalar.copy(h1_sb[:], h1[:])
+            nc.vector.tensor_tensor(h[i][:, c], h2[:], h1_sb[:], MAX)
+
+        def scatter(i, lo, hi):
+            weights = wgs_nat[:, lo:hi] if i < 4 else wgs_perm[:, i - 4, lo:hi]
+            nc.vector.tensor_tensor(page[i][:].indirect(cols(list2, lo, hi)), h[i][:, lo:hi], weights, MULT)
+
+        x1 = {}
+
+        def fetch_first(i, lo, hi):
+            if lo == 0:
+                x1[i] = work.tile([P, M], F32, name="x1")
+            nc.vector.tensor_copy(x1[i][:, lo:hi], page[i][:].indirect(cols(list3, lo, hi)))
+
+        z = {}
+
+        def fetch_second(i, lo, hi):
+            if lo == 0:
+                z[i] = work.tile([P, M], F32, name="z")
+            nc.vector.tensor_tensor(z[i][:, lo:hi], page[i][:].indirect(cols(list4, lo, hi)), x1[i][:, lo:hi], MULT)
+            if i < 4:
+                zb = work.tile([P, M], BF16, name="zb")
+                nc.scalar.activation(zb[:], z[i][:], COPY, scale=gain_nat[:, i : i + 1])
+                for t in range(PACK):
+                    nc.sync.dma_start(planes[32 * i : 32 * (i + 1), t, :], zb[t:P:PACK, :])
+            else:
+                t = i - 4
+                nc.scalar.activation(z_grouped[:, lo:hi, t], z[i][:, lo:hi], COPY, scale=gain_perm[:, t : t + 1])
+
+        first_stage(0, 0)
+        scatter(0, 0, BANK)
+        w1_grouped[1] = load_w1_natural(1)
+        list3 = load_list("list3", offs3)
+        list4 = load_list("list4", offs4)
+        gain_nat = held.tile([P, 4], F32)
+        with nc.allow_non_contiguous_dma(reason="one value a partition"):
+            nc.sync.dma_start(gain_nat[:], gain[0:K_PASS].rearrange("(c p) -> p c", p=P))
+        w1_grouped[2] = load_w1_natural(2)
+        page[1] = load_page(1)
+        first_stage(0, 1)
+        quantize(w1c_nat[1][:], w1s_nat[1][:], w1_grouped[1])
+        scatter(0, BANK, S)
+        fetch_first(0, 0, M)
+        first_stage(1, 0)
+        first_stage(1, 1)
+
+        planes = big.tile([P, PACK, M], BF16, name="big", align_bytes=64)
+        z_grouped = held.tile([P, M, PACK], BF16, align_bytes=64)
+        wgs_perm = held.tile([P, PACK, S], F32)
+        gain_perm = held.tile([P, PACK], F32)
+        rel_sb = held.tile([P, N // P], F32)
+
+        for i in range(1, TILES):
+            if i + 1 < 4:
+                quantize(w1c_nat[i + 1][:], w1s_nat[i + 1][:], w1_grouped[i + 1])
+            if i + 2 < 4:
+                w1_grouped[i + 2] = load_w1_natural(i + 2)
+            if i + 2 == 4:
+                w1_perm = [load_rows(w1[K_PASS * a : K_PASS * (a + 1), K_PASS:], True) for a in range(2)]
+            if i + 1 == 4:
+                for a in range(2):
+                    quantize(w1c_perm[a][:], w1s_perm[a][:], w1_perm[a])
+                for q in range(4):
+                    nc.sync.dma_start(
+                        wgs_perm[32 * q : 32 * (q + 1), :, :], wgs.rearrange("(p t) s -> p t s", t=PACK)
+                    )
+                nc.sync.dma_start(gain_perm[:], gain[K_PASS:].rearrange("(p t) -> p t", t=PACK))
+            if i == 5:
+                for b in range(2):
+                    quantize(w3c[b][:], w3s[b][:], load_rows(w3[K_PASS * b : K_PASS * (b + 1), :], False))
+                with nc.allow_non_contiguous_dma(reason="one value a partition"):
+                    nc.sync.dma_start(rel_sb[:], rel.rearrange("(c p) -> p c", p=P))
+            if i == 6:
+                for half in range(2):
+                    c = slice(BANK * half, BANK * (half + 1))
+                    grouped = stage.tile([P, BANK, PACK], BF16, name="grouped", align_bytes=64)
+                    nc.scalar.copy(
+                        grouped[:].rearrange("p (c i) j -> p c j i", i=4),
+                        planes[:, :, c].rearrange("p j (c i) -> p c j i", i=4),
+                    )
+                    quantize(zc[0][:, c], zs[0][:, c], grouped[:].rearrange("p c j -> p (c j)"))
+            if i + 1 < TILES:
+                page[i + 1] = load_page(i + 1)
+            scatter(i, 0, S)
+            if i == 6:
+                first_stage(7, 0)
+                first_stage(7, 1)
+                fetch_second(5, 0, M)
+            elif i < 6:
+                fetch_second(i - 1, 0, M)
+                first_stage(i + 1, 0)
+                first_stage(i + 1, 1)
+                fetch_first(i, 0, M)
+
+        staged = big.tile([P, N // P, M], F32, name="big", align_bytes=64)
+        out_view = out.rearrange("(i p) m -> p i m", p=P)
+
+        def last_product(lo, hi):
+            width = hi - lo
+            per_bank = BANK // width
+            quantize(zc[1][:, lo:hi], zs[1][:, lo:hi], z_grouped[:, lo:hi, :].rearrange("p c j -> p (c j)"))
+            for g in range(N // P // per_bank):
+                acc = psum.tile([P, per_bank, width], F32, name="bank")
+                for b in range(2):
+                    for u in range(per_bank):
+                        n = slice(P * (g * per_bank + u), P * (g * per_bank + u + 1))
+                        nc.tensor.matmul_mx(
+                            out=acc[:, u, :], lhsT=w3c[b][:, n].bitcast(FP8X4), lhsT_scale=w3s[b][:, n],
+                            rhs=zc[b][:, lo:hi].bitcast(FP8X4), rhs_scale=zs[b][:, lo:hi],
+                            start=(b == 0 and u == 0), stop=(b == 1 and u == per_bank - 1),
+                        )
+                for u in range(per_bank):
+                    i = g * per_bank + u
+                    if per_bank > 1 and g == 1:
+                        nc.vector.tensor_scalar_mul(staged[:, i, lo:hi], acc[:, u, :], rel_sb[:, i : i + 1])
+                    else:
+                        nc.scalar.activation(staged[:, i, lo:hi], acc[:, u, :], COPY, scale=rel_sb[:, i : i + 1])
+                rows = slice(g * per_bank, (g + 1) * per_bank)
+                nc.sync.dma_start(out_view[:, rows, lo:hi], staged[:, rows, lo:hi])
+
+        previous = None
+        for lo, hi in TAIL_CHUNKS:
+            fetch_first(6, lo, hi)
+            fetch_first(7, lo, hi)
+            fetch_second(6, lo, hi)
+            fetch_second(7, lo, hi)
+            if previous is not None:
+                last_product(*previous)
+            previous = (lo, hi)
+        last_product(*previous)

@@ -22,7 +22,9 @@ PACK = 4
 K_PASS = P * PACK
 BANK = 512
 TILES = H // P
-TAIL_CHUNKS = ((0, 512), (512, 768), (768, 1024))
+CHUNK_A, CHUNK_B, CHUNK_C = (0, 512), (512, 768), (768, 1024)
+RAW_SLOT = ("z_late0", "x_before_last", "z_codes", "z_rounded")
+X_SLOT = {1: "w1_codes", 2: "w3_codes", 5: "x_before_last"}
 
 
 def tile_list_royal_succession_features_kernel(
@@ -35,6 +37,7 @@ def tile_list_royal_succession_features_kernel(
         pages = ctx.enter_context(tc.tile_pool(name="pages", bufs=5))
         stage = ctx.enter_context(tc.tile_pool(name="stage", bufs=3))
         work = ctx.enter_context(tc.tile_pool(name="work", bufs=2))
+        chain = ctx.enter_context(tc.tile_pool(name="chain", bufs=1))
         psum = ctx.enter_context(tc.psum_pool(name="psum", bufs=8))
 
         def load_list(name, src):
@@ -71,11 +74,14 @@ def tile_list_royal_succession_features_kernel(
         nc.sync.dma_start(w2w[:].bitcast(I32), w2_words.rearrange("a p c -> p a c").bitcast(I32))
 
         def load_w1_natural(c):
-            raw = stage.tile([P, 2, PACK, P], F32, name="raw")
+            raw = chain.tile([P, 2, PACK, P], F32, name=RAW_SLOT[c], align_bytes=64)
             for a in range(2):
                 rows = w1[K_PASS * a : K_PASS * (a + 1), P * c : P * (c + 1)]
                 nc.sync.dma_start(raw[:, a, :, :], rows.rearrange("(p j) c -> p j c", j=PACK))
-            grouped = stage.tile([P, 2, P, PACK], BF16, name="grouped", align_bytes=64)
+            if c == 1:
+                grouped = chain.tile([P, 2, P, PACK], BF16, name="h0_second", align_bytes=64)
+            else:
+                grouped = stage.tile([P, 2, P, PACK], BF16, name="grouped", align_bytes=64)
             for a in range(2):
                 nc.scalar.copy(
                     grouped[:, a, :, :].rearrange("p (c i) j -> p c j i", i=4),
@@ -83,21 +89,24 @@ def tile_list_royal_succession_features_kernel(
                 )
             return grouped[:].rearrange("p a c j -> p (a c j)")
 
-        def load_rows(src, permuted):
-            raw = stage.tile([P, PACK, BANK], F32, name="raw")
-            nc.sync.dma_start(raw[:], src.rearrange("(p j) c -> p j c", j=PACK))
-            grouped = stage.tile([P, BANK, PACK], BF16, name="grouped", align_bytes=64)
-            if permuted:
-                nc.scalar.copy(
-                    grouped[:].rearrange("p (t m) j -> p t m j", t=PACK),
-                    raw[:].rearrange("p j (m t) -> p t m j", t=PACK),
-                )
-            else:
-                nc.scalar.copy(
-                    grouped[:].rearrange("p (c i) j -> p c j i", i=4),
-                    raw[:].rearrange("p j (c i) -> p c j i", i=4),
-                )
-            return grouped[:].rearrange("p c j -> p (c j)")
+        def load_rows(src, permuted, slot):
+            grouped = chain.tile([P, 2, BANK, PACK], BF16, name=slot, align_bytes=64)
+            for a in range(2):
+                if a == 0:
+                    both = big.tile([P, 2, PACK, BANK], F32, name="big", align_bytes=64)
+                raw = both[:, a, :, :]
+                nc.sync.dma_start(raw[:], src[K_PASS * a : K_PASS * (a + 1), :].rearrange("(p j) c -> p j c", j=PACK))
+                if permuted:
+                    nc.scalar.copy(
+                        grouped[:, a, :, :].rearrange("p (t m) j -> p t m j", t=PACK),
+                        raw[:].rearrange("p j (m t) -> p t m j", t=PACK),
+                    )
+                else:
+                    nc.scalar.copy(
+                        grouped[:, a, :, :].rearrange("p (c i) j -> p c j i", i=4),
+                        raw[:].rearrange("p j (c i) -> p c j i", i=4),
+                    )
+            return grouped[:].rearrange("p a c j -> p (a c j)")
 
         def quantize(codes, scales, grouped):
             nc.vector.quantize_mx(out=codes.bitcast(FP8X4), scales=scales, in_=grouped)
@@ -140,12 +149,15 @@ def tile_list_royal_succession_features_kernel(
 
         w1c_nat = [held.tile([P, 2 * P], U32, name="w1c%d" % c, align_bytes=64) for c in range(4)]
         w1s_nat = [held.tile([P, 2 * P], U8, name="w1s%d" % c, align_bytes=64) for c in range(4)]
-        w1c_perm = [held.tile([P, K_PASS], U32, name="w1cp%d" % a, align_bytes=64) for a in range(2)]
-        w1s_perm = [held.tile([P, K_PASS], U8, name="w1sp%d" % a, align_bytes=64) for a in range(2)]
-        w3c = [held.tile([P, N], U32, name="w3c%d" % b, align_bytes=64) for b in range(2)]
-        w3s = [held.tile([P, N], U8, name="w3s%d" % b, align_bytes=64) for b in range(2)]
-        zc = [held.tile([P, M], U32, name="zc%d" % b, align_bytes=64) for b in range(2)]
+        codes = {}
+        w1s_perm = held.tile([P, 2 * K_PASS], U8, align_bytes=64)
+        w3s = held.tile([P, 2 * N], U8, align_bytes=64)
         zs = [held.tile([P, M], U8, name="zs%d" % b, align_bytes=64) for b in range(2)]
+        zc_late = held.tile([P, M], U32, align_bytes=64)
+
+        def quantize_into(slot, scales, grouped):
+            codes[slot] = chain.tile([P, M], U32, name=slot, align_bytes=64)
+            quantize(codes[slot][:], scales, grouped)
 
         quantize(w1c_nat[0][:], w1s_nat[0][:], w1_grouped[0])
         for half in range(2):
@@ -163,157 +175,185 @@ def tile_list_royal_succession_features_kernel(
                 )
             t = i - 4
             c1 = slice(P * t, P * (t + 1))
+            c2 = slice(K_PASS * a + P * t, K_PASS * a + P * (t + 1))
             return (
-                w1c_perm[a][:, c1].bitcast(FP8X4),
-                w1s_perm[a][:, c1],
+                codes["w1_codes"][:, c2].bitcast(FP8X4),
+                w1s_perm[:, c2],
                 w2w_perm[:, a, 2 * P * t : 2 * P * (t + 1)].bitcast(FP4X4),
                 w2s_perm[:, a, c1],
             )
 
         h = {}
+        x1 = {}
+        h_slots = [held.tile([P, S], F32, name="h%d" % u) for u in range(3)]
 
         def first_stage(i, half):
             if half == 0:
-                h[i] = work.tile([P, S], F32, name="h")
+                h[i] = x1[5] if i == 7 else h_slots[i % 3]
             c = slice(BANK * half, BANK * (half + 1))
             h1 = psum.tile([P, BANK], F32, name="bank")
             h2 = psum.tile([P, BANK], F32, name="bank")
             for a in range(2):
                 c1, s1, c2, s2 = stationary(i, a)
                 moving = v_words[a][:, c].bitcast(FP8X4)
-                for acc, codes, scales in ((h1, c1, s1), (h2, c2, s2)):
+                for acc, words, scales in ((h1, c1, s1), (h2, c2, s2)):
                     nc.tensor.matmul_mx(
-                        out=acc[:], lhsT=codes, lhsT_scale=scales, rhs=moving, rhs_scale=v_scales[:, a, c],
+                        out=acc[:], lhsT=words, lhsT_scale=scales, rhs=moving, rhs_scale=v_scales[:, a, c],
                         start=(a == 0), stop=(a == 1),
                     )
             h1_sb = stage.tile([P, BANK], F32, name="h1_sb")
             nc.scalar.copy(h1_sb[:], h1[:])
-            nc.vector.tensor_tensor(h[i][:, c], h2[:], h1_sb[:], MAX)
+            if (i, half) == (0, 1):
+                second = chain.tile([P, BANK], F32, name="h0_second", align_bytes=64)
+                h["second"] = second[:]
+            nc.vector.tensor_tensor(h["second"] if (i, half) == (0, 1) else h[i][:, c], h2[:], h1_sb[:], MAX)
 
         def scatter(i, lo, hi):
             weights = wgs_nat[:, lo:hi] if i < 4 else wgs_perm[:, i - 4, lo:hi]
-            nc.vector.tensor_tensor(page[i][:].indirect(cols(list2, lo, hi)), h[i][:, lo:hi], weights, MULT)
+            nc.vector.tensor_tensor(page[i][:].indirect(cols(list2, lo, hi)), h["second"] if lo > 0 else h[i][:, lo:hi], weights, MULT)
 
-        x1 = {}
+        def fetch_first(i, lo, hi, dst):
+            nc.vector.tensor_copy(dst, page[i][:].indirect(cols(list3, lo, hi)))
+            return dst
 
-        def fetch_first(i, lo, hi):
-            if lo == 0:
-                x1[i] = work.tile([P, M], F32, name="x1")
-            nc.vector.tensor_copy(x1[i][:, lo:hi], page[i][:].indirect(cols(list3, lo, hi)))
+        def first_tile(i, width):
+            if i in X_SLOT:
+                x = chain.tile([P, width], F32, name=X_SLOT[i], align_bytes=64)
+                return x[:]
+            x = work.tile([P, width], F32, name="x1")
+            return x[:]
 
-        z = {}
-
-        def fetch_second(i, lo, hi):
-            if lo == 0:
-                z[i] = work.tile([P, M], F32, name="z")
-            nc.vector.tensor_tensor(z[i][:, lo:hi], page[i][:].indirect(cols(list4, lo, hi)), x1[i][:, lo:hi], MULT)
+        def fetch_second(i, lo, hi, first):
+            if i == 5:
+                z = chain.tile([P, hi - lo], F32, name="z_rounded", align_bytes=64)
+            elif i < 5 or (i == 6 and lo == 0):
+                z = h[i + 1][:, 0 : hi - lo]
+            else:
+                z = stage.tile([P, hi - lo], F32, name="z_tail")
+            nc.vector.tensor_tensor(z[:], page[i][:].indirect(cols(list4, lo, hi)), first, MULT)
             if i < 4:
                 zb = work.tile([P, M], BF16, name="zb")
-                nc.scalar.activation(zb[:], z[i][:], COPY, scale=gain_nat[:, i : i + 1])
+                nc.scalar.activation(zb[:], z[:], COPY, scale=gain_nat[:, i : i + 1])
                 for t in range(PACK):
                     nc.sync.dma_start(planes[32 * i : 32 * (i + 1), t, :], zb[t:P:PACK, :])
             else:
                 t = i - 4
-                nc.scalar.activation(z_grouped[:, lo:hi, t], z[i][:, lo:hi], COPY, scale=gain_perm[:, t : t + 1])
+                for c_lo, c_hi in (CHUNK_A, CHUNK_B, CHUNK_C):
+                    if lo <= c_lo and c_hi <= hi:
+                        nc.scalar.activation(
+                            z_grouped[c_lo][:, :, t], z[:, c_lo - lo : c_hi - lo], COPY, scale=gain_perm[:, t : t + 1]
+                        )
 
         first_stage(0, 0)
         scatter(0, 0, BANK)
         w1_grouped[1] = load_w1_natural(1)
         list3 = load_list("list3", offs3)
         list4 = load_list("list4", offs4)
+        w1_grouped[2] = load_w1_natural(2)
+        page[1] = load_page(1)
         gain_nat = held.tile([P, 4], F32)
         with nc.allow_non_contiguous_dma(reason="one value a partition"):
             nc.sync.dma_start(gain_nat[:], gain[0:K_PASS].rearrange("(c p) -> p c", p=P))
-        w1_grouped[2] = load_w1_natural(2)
-        page[1] = load_page(1)
-        first_stage(0, 1)
         quantize(w1c_nat[1][:], w1s_nat[1][:], w1_grouped[1])
+        first_stage(0, 1)
         scatter(0, BANK, S)
-        fetch_first(0, 0, M)
+        x1[0] = fetch_first(0, 0, M, first_tile(0, M))
         first_stage(1, 0)
         first_stage(1, 1)
 
-        planes = big.tile([P, PACK, M], BF16, name="big", align_bytes=64)
-        z_grouped = held.tile([P, M, PACK], BF16, align_bytes=64)
+        planes = held.tile([P, PACK, M], BF16, align_bytes=64)
+        z_grouped = {
+            lo: chain.tile([P, hi - lo, PACK], BF16, name="z_late%d" % lo, align_bytes=64)
+            for lo, hi in (CHUNK_A, CHUNK_B, CHUNK_C)
+        }
         wgs_perm = held.tile([P, PACK, S], F32)
         gain_perm = held.tile([P, PACK], F32)
         rel_sb = held.tile([P, N // P], F32)
 
-        for i in range(1, TILES):
+        for i in range(1, TILES - 1):
             if i + 1 < 4:
                 quantize(w1c_nat[i + 1][:], w1s_nat[i + 1][:], w1_grouped[i + 1])
-            if i + 2 < 4:
-                w1_grouped[i + 2] = load_w1_natural(i + 2)
-            if i + 2 == 4:
-                w1_perm = [load_rows(w1[K_PASS * a : K_PASS * (a + 1), K_PASS:], True) for a in range(2)]
-            if i + 1 == 4:
-                for a in range(2):
-                    quantize(w1c_perm[a][:], w1s_perm[a][:], w1_perm[a])
+            if i == 1:
+                w1_grouped[3] = load_w1_natural(3)
+                w1_perm = load_rows(w1[:, K_PASS:], True, "w1_rounded")
+                w3_grouped = load_rows(w3, False, "w3_rounded")
+            if i >= 3:
                 for q in range(4):
                     nc.sync.dma_start(
-                        wgs_perm[32 * q : 32 * (q + 1), :, :], wgs.rearrange("(p t) s -> p t s", t=PACK)
+                        wgs_perm[32 * q : 32 * (q + 1), i - 3, :], wgs.rearrange("(p t) s -> t p s", t=PACK)[i - 3]
                     )
+            if i == 3:
                 nc.sync.dma_start(gain_perm[:], gain[K_PASS:].rearrange("(p t) -> p t", t=PACK))
-            if i == 5:
-                for b in range(2):
-                    quantize(w3c[b][:], w3s[b][:], load_rows(w3[K_PASS * b : K_PASS * (b + 1), :], False))
+            page[i + 1] = load_page(i + 1)
+            if i == 6:
                 with nc.allow_non_contiguous_dma(reason="one value a partition"):
                     nc.sync.dma_start(rel_sb[:], rel.rearrange("(c p) -> p c", p=P))
+            scatter(i, 0, S)
+            if i < 6:
+                first_stage(i + 1, 0)
             if i == 6:
+                grouped = chain.tile([P, M, PACK], BF16, name="z_rounded", align_bytes=64)
                 for half in range(2):
                     c = slice(BANK * half, BANK * (half + 1))
-                    grouped = stage.tile([P, BANK, PACK], BF16, name="grouped", align_bytes=64)
                     nc.scalar.copy(
-                        grouped[:].rearrange("p (c i) j -> p c j i", i=4),
+                        grouped[:, c, :].rearrange("p (c i) j -> p c j i", i=4),
                         planes[:, :, c].rearrange("p j (c i) -> p c j i", i=4),
                     )
-                    quantize(zc[0][:, c], zs[0][:, c], grouped[:].rearrange("p c j -> p (c j)"))
-            if i + 1 < TILES:
-                page[i + 1] = load_page(i + 1)
-            scatter(i, 0, S)
+                quantize_into("z_codes", zs[0][:], grouped[:].rearrange("p c j -> p (c j)"))
+            fetch_second(i - 1, 0, M, x1[i - 1])
+            if i == 2:
+                quantize_into("w1_codes", w1s_perm[:], w1_perm)
+            if i == 3:
+                quantize_into("w3_codes", w3s[:], w3_grouped)
             if i == 6:
-                first_stage(7, 0)
-                first_stage(7, 1)
-                fetch_second(5, 0, M)
-            elif i < 6:
-                fetch_second(i - 1, 0, M)
                 first_stage(i + 1, 0)
-                first_stage(i + 1, 1)
-                fetch_first(i, 0, M)
+            first_stage(i + 1, 1)
+            width = M if i < 6 else BANK
+            x1[i] = fetch_first(i, 0, width, first_tile(i, width))
 
         staged = big.tile([P, N // P, M], F32, name="big", align_bytes=64)
         out_view = out.rearrange("(i p) m -> p i m", p=P)
+        zc = [codes["z_codes"], zc_late]
 
         def last_product(lo, hi):
             width = hi - lo
             per_bank = BANK // width
-            quantize(zc[1][:, lo:hi], zs[1][:, lo:hi], z_grouped[:, lo:hi, :].rearrange("p c j -> p (c j)"))
+            quantize(zc[1][:, lo:hi], zs[1][:, lo:hi], z_grouped[lo][:].rearrange("p c j -> p (c j)"))
             for g in range(N // P // per_bank):
                 acc = psum.tile([P, per_bank, width], F32, name="bank")
                 for b in range(2):
                     for u in range(per_bank):
-                        n = slice(P * (g * per_bank + u), P * (g * per_bank + u + 1))
+                        first = N * b + P * (g * per_bank + u)
+                        n = slice(first, first + P)
                         nc.tensor.matmul_mx(
-                            out=acc[:, u, :], lhsT=w3c[b][:, n].bitcast(FP8X4), lhsT_scale=w3s[b][:, n],
+                            out=acc[:, u, :], lhsT=codes["w3_codes"][:, n].bitcast(FP8X4), lhsT_scale=w3s[:, n],
                             rhs=zc[b][:, lo:hi].bitcast(FP8X4), rhs_scale=zs[b][:, lo:hi],
                             start=(b == 0 and u == 0), stop=(b == 1 and u == per_bank - 1),
                         )
                 for u in range(per_bank):
                     i = g * per_bank + u
-                    if per_bank > 1 and g == 1:
+                    if i >= 2:
                         nc.vector.tensor_scalar_mul(staged[:, i, lo:hi], acc[:, u, :], rel_sb[:, i : i + 1])
                     else:
                         nc.scalar.activation(staged[:, i, lo:hi], acc[:, u, :], COPY, scale=rel_sb[:, i : i + 1])
                 rows = slice(g * per_bank, (g + 1) * per_bank)
                 nc.sync.dma_start(out_view[:, rows, lo:hi], staged[:, rows, lo:hi])
 
-        previous = None
-        for lo, hi in TAIL_CHUNKS:
-            fetch_first(6, lo, hi)
-            fetch_first(7, lo, hi)
-            fetch_second(6, lo, hi)
-            fetch_second(7, lo, hi)
-            if previous is not None:
-                last_product(*previous)
-            previous = (lo, hi)
-        last_product(*previous)
+        scatter(7, 0, S)
+        fetch_second(6, *CHUNK_A, x1[6])
+        x7 = first_tile(7, CHUNK_B[1])
+        fetch_first(7, *CHUNK_A, x7[:, 0:BANK])
+        x6 = chain.tile([P, CHUNK_B[1] - CHUNK_B[0]], F32, name="z_rounded", align_bytes=64)
+        fetch_first(6, *CHUNK_B, x6[:])
+        fetch_second(7, *CHUNK_A, x7[:, 0:BANK])
+        fetch_first(7, *CHUNK_B, x7[:, BANK:])
+        fetch_second(6, *CHUNK_B, x6[:])
+        fetch_second(7, *CHUNK_B, x7[:, BANK:])
+        last_product(*CHUNK_A)
+        x_last = chain.tile([P, 2, CHUNK_C[1] - CHUNK_C[0]], F32, name="z_late0", align_bytes=64)
+        fetch_first(6, *CHUNK_C, x_last[:, 0, :])
+        fetch_first(7, *CHUNK_C, x_last[:, 1, :])
+        fetch_second(6, *CHUNK_C, x_last[:, 0, :])
+        fetch_second(7, *CHUNK_C, x_last[:, 1, :])
+        last_product(*CHUNK_B)
+        last_product(*CHUNK_C)

@@ -24,7 +24,7 @@ BANK = 512
 TILES = H // P
 CHUNK_A, CHUNK_B, CHUNK_C = (0, 512), (512, 768), (768, 1024)
 RAW_SLOT = ("z_late0", "x_before_last", "z_codes", "z_rounded")
-X_SLOT = {1: "w1_codes", 2: "w3_codes", 5: "x_before_last"}
+X_SLOT = {1: "w1_codes", 3: "w3_codes", 5: "x_before_last"}
 
 
 def tile_list_royal_succession_features_kernel(
@@ -70,8 +70,6 @@ def tile_list_royal_succession_features_kernel(
             return t
 
         tab0 = load_table(0)
-        w2w = held.tile([P, 2, 2 * H], U8, align_bytes=64)
-        nc.sync.dma_start(w2w[:].bitcast(I32), w2_words.rearrange("a p c -> p a c").bitcast(I32))
 
         def load_w1_natural(c):
             raw = chain.tile([P, 2, PACK, P], F32, name=RAW_SLOT[c], align_bytes=64)
@@ -98,8 +96,8 @@ def tile_list_royal_succession_features_kernel(
                 nc.sync.dma_start(raw[:], src[K_PASS * a : K_PASS * (a + 1), :].rearrange("(p j) c -> p j c", j=PACK))
                 if permuted:
                     nc.scalar.copy(
-                        grouped[:, a, :, :].rearrange("p (t m) j -> p t m j", t=PACK),
-                        raw[:].rearrange("p j (m t) -> p t m j", t=PACK),
+                        grouped[:, a, :, :].rearrange("p (t m) j -> p m t j", t=PACK),
+                        raw[:].rearrange("p j (m t) -> p m t j", t=PACK),
                     )
                 else:
                     nc.scalar.copy(
@@ -121,11 +119,14 @@ def tile_list_royal_succession_features_kernel(
             return t
 
         w1_grouped = {0: load_w1_natural(0)}
-        tab1 = load_table(1)
         list2 = load_list("list2", offs2)
+        tab1 = load_table(1)
+        w2w = held.tile([P, 2, 2 * H], U8, align_bytes=64)
+        nc.sync.dma_start(w2w[:].bitcast(I32), w2_words.rearrange("a p c -> p a c").bitcast(I32))
         wgs_nat = held.tile([P, S], F32)
-        nc.sync.dma_start(wgs_nat[:], wgs)
+        nc.sync.dma_start(wgs_nat[:, 0:BANK], wgs[:, 0:BANK])
         page = {0: load_page(0)}
+        nc.sync.dma_start(wgs_nat[:, BANK:], wgs[:, BANK:])
 
         picked_scales = held.tile([P, S], U8, align_bytes=64)
         nc.vector.tensor_copy(picked_scales[:], scale_rows[:].indirect(list1[:]))
@@ -136,11 +137,6 @@ def tile_list_royal_succession_features_kernel(
         v_words = [held.tile([P, S], U32, name="v_words%d" % a, align_bytes=64) for a in range(2)]
         nc.vector.tensor_copy(v_words[0][:], tab0[:].indirect(list1[:]))
 
-        w2w_perm = held.tile([P, 2, H], U8, align_bytes=64)
-        nc.vector.tensor_copy(
-            w2w_perm[:].bitcast(U16).rearrange("p a (t m) -> p a t m", t=PACK),
-            w2w[:, :, H:].bitcast(U16).rearrange("p a (m t) -> p a t m", t=PACK),
-        )
         w2s_perm = held.tile([P, 2, K_PASS], U8, align_bytes=64)
         nc.vector.tensor_copy(
             w2s_perm[:].rearrange("p a (t m) -> p a t m", t=PACK),
@@ -163,6 +159,11 @@ def tile_list_royal_succession_features_kernel(
         for half in range(2):
             lo, hi = BANK * half, BANK * (half + 1)
             nc.vector.tensor_copy(v_words[1][:, lo:hi], tab1[:].indirect(cols(list1, lo, hi)))
+        w2w_perm = held.tile([P, 2, H], U8, align_bytes=64)
+        nc.vector.tensor_copy(
+            w2w_perm[:].bitcast(U16).rearrange("p a (t m) -> p a t m", t=PACK),
+            w2w[:, :, H:].bitcast(U16).rearrange("p a (m t) -> p a t m", t=PACK),
+        )
 
         def stationary(i, a):
             if i < 4:
@@ -193,10 +194,10 @@ def tile_list_royal_succession_features_kernel(
             c = slice(BANK * half, BANK * (half + 1))
             h1 = psum.tile([P, BANK], F32, name="bank")
             h2 = psum.tile([P, BANK], F32, name="bank")
-            for a in range(2):
-                c1, s1, c2, s2 = stationary(i, a)
-                moving = v_words[a][:, c].bitcast(FP8X4)
-                for acc, words, scales in ((h1, c1, s1), (h2, c2, s2)):
+            for acc, u in ((h1, 0), (h2, 2)):
+                for a in range(2):
+                    words, scales = stationary(i, a)[u : u + 2]
+                    moving = v_words[a][:, c].bitcast(FP8X4)
                     nc.tensor.matmul_mx(
                         out=acc[:], lhsT=words, lhsT_scale=scales, rhs=moving, rhs_scale=v_scales[:, a, c],
                         start=(a == 0), stop=(a == 1),
@@ -226,8 +227,10 @@ def tile_list_royal_succession_features_kernel(
         def fetch_second(i, lo, hi, first):
             if i == 5:
                 z = chain.tile([P, hi - lo], F32, name="z_rounded", align_bytes=64)
-            elif i < 5 or (i == 6 and lo == 0):
+            elif i == 1 or (i == 6 and lo == 0):
                 z = h[i + 1][:, 0 : hi - lo]
+            elif i < 5:
+                z = h[i][:, 0 : hi - lo]
             else:
                 z = stage.tile([P, hi - lo], F32, name="z_tail")
             nc.vector.tensor_tensor(z[:], page[i][:].indirect(cols(list4, lo, hi)), first, MULT)
@@ -239,9 +242,11 @@ def tile_list_royal_succession_features_kernel(
             else:
                 t = i - 4
                 for c_lo, c_hi in (CHUNK_A, CHUNK_B, CHUNK_C):
-                    if lo <= c_lo and c_hi <= hi:
+                    a, b = max(lo, c_lo), min(hi, c_hi)
+                    if a < b:
                         nc.scalar.activation(
-                            z_grouped[c_lo][:, :, t], z[:, c_lo - lo : c_hi - lo], COPY, scale=gain_perm[:, t : t + 1]
+                            z_grouped[c_lo][:, a - c_lo : b - c_lo, t], z[:, a - lo : b - lo], COPY,
+                            scale=gain_perm[:, t : t + 1],
                         )
 
         first_stage(0, 0)
@@ -276,7 +281,6 @@ def tile_list_royal_succession_features_kernel(
             if i == 1:
                 w1_grouped[3] = load_w1_natural(3)
                 w1_perm = load_rows(w1[:, K_PASS:], True, "w1_rounded")
-                w3_grouped = load_rows(w3, False, "w3_rounded")
             if i >= 3:
                 for q in range(4):
                     nc.sync.dma_start(
@@ -285,6 +289,8 @@ def tile_list_royal_succession_features_kernel(
             if i == 3:
                 nc.sync.dma_start(gain_perm[:], gain[K_PASS:].rearrange("(p t) -> p t", t=PACK))
             page[i + 1] = load_page(i + 1)
+            if i == 2:
+                w3_grouped = load_rows(w3, False, "w3_rounded")
             if i == 6:
                 with nc.allow_non_contiguous_dma(reason="one value a partition"):
                     nc.sync.dma_start(rel_sb[:], rel.rearrange("(c p) -> p c", p=P))
@@ -301,24 +307,25 @@ def tile_list_royal_succession_features_kernel(
                     )
                 quantize_into("z_codes", zs[0][:], grouped[:].rearrange("p c j -> p (c j)"))
             fetch_second(i - 1, 0, M, x1[i - 1])
-            if i == 2:
-                quantize_into("w1_codes", w1s_perm[:], w1_perm)
-            if i == 3:
-                quantize_into("w3_codes", w3s[:], w3_grouped)
             if i == 6:
                 first_stage(i + 1, 0)
             first_stage(i + 1, 1)
             width = M if i < 6 else BANK
             x1[i] = fetch_first(i, 0, width, first_tile(i, width))
+            if i == 2:
+                quantize_into("w1_codes", w1s_perm[:], w1_perm)
+            if i == 4:
+                quantize_into("w3_codes", w3s[:], w3_grouped)
 
         staged = big.tile([P, N // P, M], F32, name="big", align_bytes=64)
         out_view = out.rearrange("(i p) m -> p i m", p=P)
         zc = [codes["z_codes"], zc_late]
 
-        def last_product(lo, hi):
+        def last_product(lo, hi, base):
             width = hi - lo
-            per_bank = BANK // width
-            quantize(zc[1][:, lo:hi], zs[1][:, lo:hi], z_grouped[lo][:].rearrange("p c j -> p (c j)"))
+            per_bank = 1 if width == BANK else 2
+            rounded = z_grouped[base][:, lo - base : hi - base, :]
+            quantize(zc[1][:, lo:hi], zs[1][:, lo:hi], rounded.rearrange("p c j -> p (c j)"))
             for g in range(N // P // per_bank):
                 acc = psum.tile([P, per_bank, width], F32, name="bank")
                 for b in range(2):
@@ -340,20 +347,23 @@ def tile_list_royal_succession_features_kernel(
                 nc.sync.dma_start(out_view[:, rows, lo:hi], staged[:, rows, lo:hi])
 
         scatter(7, 0, S)
+        x6 = chain.tile([P, CHUNK_B[1] - CHUNK_B[0]], F32, name="z_rounded", align_bytes=64)
+        fetch_first(6, *CHUNK_B, x6[:])
         fetch_second(6, *CHUNK_A, x1[6])
         x7 = first_tile(7, CHUNK_B[1])
         fetch_first(7, *CHUNK_A, x7[:, 0:BANK])
-        x6 = chain.tile([P, CHUNK_B[1] - CHUNK_B[0]], F32, name="z_rounded", align_bytes=64)
-        fetch_first(6, *CHUNK_B, x6[:])
+        fetch_second(6, *CHUNK_B, x6[:])
         fetch_second(7, *CHUNK_A, x7[:, 0:BANK])
         fetch_first(7, *CHUNK_B, x7[:, BANK:])
-        fetch_second(6, *CHUNK_B, x6[:])
-        fetch_second(7, *CHUNK_B, x7[:, BANK:])
-        last_product(*CHUNK_A)
-        x_last = chain.tile([P, 2, CHUNK_C[1] - CHUNK_C[0]], F32, name="z_late0", align_bytes=64)
-        fetch_first(6, *CHUNK_C, x_last[:, 0, :])
+        x_last = chain.tile([P, 2, CHUNK_C[1] - CHUNK_C[0]], F32, name="w3_rounded", align_bytes=64)
         fetch_first(7, *CHUNK_C, x_last[:, 1, :])
-        fetch_second(6, *CHUNK_C, x_last[:, 0, :])
-        fetch_second(7, *CHUNK_C, x_last[:, 1, :])
-        last_product(*CHUNK_B)
-        last_product(*CHUNK_C)
+        fetch_second(7, *CHUNK_B, x7[:, BANK:])
+        last_product(*CHUNK_A, CHUNK_A[0])
+        x6_last = chain.tile([P, CHUNK_C[1] - CHUNK_C[0]], F32, name="z_late0", align_bytes=64)
+        fetch_first(6, *CHUNK_C, x6_last[:])
+        fetch_second(7, 768, 896, x_last[:, 1, 0:P])
+        fetch_second(6, *CHUNK_C, x6_last[:])
+        last_product(*CHUNK_B, CHUNK_B[0])
+        fetch_second(7, 896, 1024, x_last[:, 1, P:])
+        last_product(768, 896, CHUNK_C[0])
+        last_product(896, 1024, CHUNK_C[0])

@@ -21,10 +21,16 @@ P = 128
 PACK = 4
 K_PASS = P * PACK
 BANK = 512
-TILES = H // P
-CHUNK_A, CHUNK_B, CHUNK_C = (0, 512), (512, 768), (768, 1024)
-RAW_SLOT = ("z_late0", "x_before_last", "z_codes", "z_rounded")
-X_SLOT = {1: "w1_codes", 3: "w3_codes", 5: "x_before_last"}
+QUADS = 4
+PLAIN_TILES = 4
+LAST = H // P - 1
+RUN = 4
+
+PART_A, PART_B, PART_C = (0, 512), (512, 768), (768, 1024)
+PART_C1, PART_C2 = (768, 896), (896, 1024)
+
+W1_STAGING = ("z_words0", "x5", "z_codes", "z_rounded")
+FIRST_READ_BYTES = {1: "w1_codes", 3: "w3_codes", 5: "x5"}
 
 
 def tile_list_royal_succession_features_kernel(
@@ -37,16 +43,74 @@ def tile_list_royal_succession_features_kernel(
         pages = ctx.enter_context(tc.tile_pool(name="pages", bufs=5))
         stage = ctx.enter_context(tc.tile_pool(name="stage", bufs=3))
         work = ctx.enter_context(tc.tile_pool(name="work", bufs=2))
-        chain = ctx.enter_context(tc.tile_pool(name="chain", bufs=1))
+        shared = ctx.enter_context(tc.tile_pool(name="shared", bufs=1))
         psum = ctx.enter_context(tc.psum_pool(name="psum", bufs=8))
 
         def load_list(name, src):
-            t = held.tile([P, S // 16], U16, name=name)
-            nc.sync.dma_start(t[:], src)
-            return t
+            lst = held.tile([P, S // 16], U16, name=name)
+            nc.sync.dma_start(lst[:], src)
+            return lst
 
-        def cols(lst, lo, hi):
+        def entries(lst, lo, hi):
             return lst[:, lo // 16 : hi // 16]
+
+        def load_table(a):
+            words = big.tile([P, T], U32, name="big", align_bytes=64)
+            nc.sync.dma_start(words[:].bitcast(I32), tab_words[a].rearrange("p t i -> p (t i)").bitcast(I32))
+            return words
+
+        def interleave(dst, src):
+            nc.scalar.copy(dst.rearrange("p (c i) j -> p c j i", i=RUN), src.rearrange("p j (c i) -> p c j i", i=RUN))
+
+        def load_w1_tile(i):
+            raw = shared.tile([P, 2, PACK, P], F32, name=W1_STAGING[i], align_bytes=64)
+            for a in range(2):
+                rows = w1[K_PASS * a : K_PASS * (a + 1), P * i : P * (i + 1)]
+                nc.sync.dma_start(raw[:, a, :, :], rows.rearrange("(p j) c -> p j c", j=PACK))
+            if i == 1:
+                rounded = shared.tile([P, 2, P, PACK], BF16, name="h0_second", align_bytes=64)
+            else:
+                rounded = stage.tile([P, 2, P, PACK], BF16, name="w1_rounded_tile", align_bytes=64)
+            for a in range(2):
+                interleave(rounded[:, a, :, :], raw[:, a, :, :])
+            return rounded[:].rearrange("p a c j -> p (a c j)")
+
+        def load_weight(src, name, reorder_columns):
+            rounded = shared.tile([P, 2, BANK, PACK], BF16, name=name, align_bytes=64)
+            raw = big.tile([P, 2, PACK, BANK], F32, name="big", align_bytes=64)
+            for a in range(2):
+                rows = src[K_PASS * a : K_PASS * (a + 1), :]
+                nc.sync.dma_start(raw[:, a, :, :], rows.rearrange("(p j) c -> p j c", j=PACK))
+                if reorder_columns:
+                    nc.scalar.copy(
+                        rounded[:, a, :, :].rearrange("p (t m) j -> p m t j", t=PACK),
+                        raw[:, a, :, :].rearrange("p j (m t) -> p m t j", t=PACK),
+                    )
+                else:
+                    interleave(rounded[:, a, :, :], raw[:, a, :, :])
+            return rounded[:].rearrange("p a c j -> p (a c j)")
+
+        def load_page(i):
+            tile = pages.tile([P, T2], F32, name="page")
+            if i < PLAIN_TILES:
+                rows = page0[P * i : P * (i + 1), :]
+            else:
+                rows = page0[K_PASS:, :].rearrange("(p t) c -> t p c", t=PACK)[i - PLAIN_TILES]
+            nc.sync.dma_start(tile[:], rows)
+            return tile
+
+        def load_per_partition(dst, src):
+            with nc.allow_non_contiguous_dma(reason="one value a partition"):
+                nc.sync.dma_start(dst, src.rearrange("(c p) -> p c", p=P))
+
+        def quantize(words, scales, rounded):
+            nc.vector.quantize_mx(out=words.bitcast(FP8X4), scales=scales, in_=rounded)
+
+        codes = {}
+
+        def quantize_shared(name, scales, rounded):
+            codes[name] = shared.tile([P, M], U32, name=name, align_bytes=64)
+            quantize(codes[name][:], scales, rounded)
 
         scale_rows = held.tile([P, T], U8, align_bytes=64)
         nc.vector.memset(scale_rows[32:64, :].bitcast(I32), 0)
@@ -55,7 +119,7 @@ def tile_list_royal_succession_features_kernel(
         nc.gpsimd.memset(w2s[:].rearrange("p a c -> p (a c)").bitcast(I32), 0)
         v_scales = held.tile([P, 2, S], U8, align_bytes=64)
         nc.vector.memset(v_scales[:].rearrange("p a c -> p (a c)").bitcast(I32), 0)
-        for q in range(4):
+        for q in range(QUADS):
             nc.gpsimd.dma_start(
                 w2s[32 * q : 32 * q + 4, :, :].bitcast(I32),
                 w2_scales[:, 4 * q : 4 * q + 4, :].rearrange("a r c -> r a c").bitcast(I32),
@@ -63,307 +127,238 @@ def tile_list_royal_succession_features_kernel(
 
         list1 = load_list("list1", offs)
         nc.sync.dma_start(scale_rows[0:32, :].bitcast(I32), tab_scales.rearrange("a q t -> q a t").bitcast(I32))
-
-        def load_table(a):
-            t = big.tile([P, T], U32, name="big", align_bytes=64)
-            nc.sync.dma_start(t[:].bitcast(I32), tab_words[a].rearrange("p t i -> p (t i)").bitcast(I32))
-            return t
-
-        tab0 = load_table(0)
-
-        def load_w1_natural(c):
-            raw = chain.tile([P, 2, PACK, P], F32, name=RAW_SLOT[c], align_bytes=64)
-            for a in range(2):
-                rows = w1[K_PASS * a : K_PASS * (a + 1), P * c : P * (c + 1)]
-                nc.sync.dma_start(raw[:, a, :, :], rows.rearrange("(p j) c -> p j c", j=PACK))
-            if c == 1:
-                grouped = chain.tile([P, 2, P, PACK], BF16, name="h0_second", align_bytes=64)
-            else:
-                grouped = stage.tile([P, 2, P, PACK], BF16, name="grouped", align_bytes=64)
-            for a in range(2):
-                nc.scalar.copy(
-                    grouped[:, a, :, :].rearrange("p (c i) j -> p c j i", i=4),
-                    raw[:, a, :, :].rearrange("p j (c i) -> p c j i", i=4),
-                )
-            return grouped[:].rearrange("p a c j -> p (a c j)")
-
-        def load_rows(src, permuted, slot):
-            grouped = chain.tile([P, 2, BANK, PACK], BF16, name=slot, align_bytes=64)
-            for a in range(2):
-                if a == 0:
-                    both = big.tile([P, 2, PACK, BANK], F32, name="big", align_bytes=64)
-                raw = both[:, a, :, :]
-                nc.sync.dma_start(raw[:], src[K_PASS * a : K_PASS * (a + 1), :].rearrange("(p j) c -> p j c", j=PACK))
-                if permuted:
-                    nc.scalar.copy(
-                        grouped[:, a, :, :].rearrange("p (t m) j -> p m t j", t=PACK),
-                        raw[:].rearrange("p j (m t) -> p m t j", t=PACK),
-                    )
-                else:
-                    nc.scalar.copy(
-                        grouped[:, a, :, :].rearrange("p (c i) j -> p c j i", i=4),
-                        raw[:].rearrange("p j (c i) -> p c j i", i=4),
-                    )
-            return grouped[:].rearrange("p a c j -> p (a c j)")
-
-        def quantize(codes, scales, grouped):
-            nc.vector.quantize_mx(out=codes.bitcast(FP8X4), scales=scales, in_=grouped)
-
-        def load_page(i):
-            t = pages.tile([P, T2], F32, name="page")
-            if i < 4:
-                src = page0[P * i : P * (i + 1), :]
-            else:
-                src = page0[K_PASS:, :].rearrange("(p t) c -> t p c", t=PACK)[i - 4]
-            nc.sync.dma_start(t[:], src)
-            return t
-
-        w1_grouped = {0: load_w1_natural(0)}
+        table0 = load_table(0)
+        w1_rounded = {0: load_w1_tile(0)}
         list2 = load_list("list2", offs2)
-        tab1 = load_table(1)
+        table1 = load_table(1)
         w2w = held.tile([P, 2, 2 * H], U8, align_bytes=64)
         nc.sync.dma_start(w2w[:].bitcast(I32), w2_words.rearrange("a p c -> p a c").bitcast(I32))
-        wgs_nat = held.tile([P, S], F32)
-        nc.sync.dma_start(wgs_nat[:, 0:BANK], wgs[:, 0:BANK])
+        wgs_plain = held.tile([P, S], F32)
+        nc.sync.dma_start(wgs_plain[:, 0:BANK], wgs[:, 0:BANK])
         page = {0: load_page(0)}
-        nc.sync.dma_start(wgs_nat[:, BANK:], wgs[:, BANK:])
 
         picked_scales = held.tile([P, S], U8, align_bytes=64)
         nc.vector.tensor_copy(picked_scales[:], scale_rows[:].indirect(list1[:]))
-        for q in range(4):
+        for q in range(QUADS):
             nc.scalar.dma_start(
                 v_scales[32 * q : 32 * q + 4, :, :].bitcast(I32), picked_scales[8 * q : 8 * q + 8, :].bitcast(I32)
             )
         v_words = [held.tile([P, S], U32, name="v_words%d" % a, align_bytes=64) for a in range(2)]
-        nc.vector.tensor_copy(v_words[0][:], tab0[:].indirect(list1[:]))
+        nc.vector.tensor_copy(v_words[0][:], table0[:].indirect(list1[:]))
 
-        w2s_perm = held.tile([P, 2, K_PASS], U8, align_bytes=64)
+        w2s_reordered = held.tile([P, 2, K_PASS], U8, align_bytes=64)
         nc.vector.tensor_copy(
-            w2s_perm[:].rearrange("p a (t m) -> p a t m", t=PACK),
+            w2s_reordered[:].rearrange("p a (t m) -> p a t m", t=PACK),
             w2s[:, :, K_PASS:].rearrange("p a (m t) -> p a t m", t=PACK),
         )
 
-        w1c_nat = [held.tile([P, 2 * P], U32, name="w1c%d" % c, align_bytes=64) for c in range(4)]
-        w1s_nat = [held.tile([P, 2 * P], U8, name="w1s%d" % c, align_bytes=64) for c in range(4)]
-        codes = {}
-        w1s_perm = held.tile([P, 2 * K_PASS], U8, align_bytes=64)
+        w1c_plain = [held.tile([P, 2 * P], U32, name="w1c%d" % i, align_bytes=64) for i in range(PLAIN_TILES)]
+        w1s_plain = [held.tile([P, 2 * P], U8, name="w1s%d" % i, align_bytes=64) for i in range(PLAIN_TILES)]
+        w1s_reordered = held.tile([P, 2 * K_PASS], U8, align_bytes=64)
         w3s = held.tile([P, 2 * N], U8, align_bytes=64)
         zs = [held.tile([P, M], U8, name="zs%d" % b, align_bytes=64) for b in range(2)]
-        zc_late = held.tile([P, M], U32, align_bytes=64)
+        z_codes1 = held.tile([P, M], U32, align_bytes=64)
 
-        def quantize_into(slot, scales, grouped):
-            codes[slot] = chain.tile([P, M], U32, name=slot, align_bytes=64)
-            quantize(codes[slot][:], scales, grouped)
-
-        quantize(w1c_nat[0][:], w1s_nat[0][:], w1_grouped[0])
-        for half in range(2):
-            lo, hi = BANK * half, BANK * (half + 1)
-            nc.vector.tensor_copy(v_words[1][:, lo:hi], tab1[:].indirect(cols(list1, lo, hi)))
-        w2w_perm = held.tile([P, 2, H], U8, align_bytes=64)
+        quantize(w1c_plain[0][:], w1s_plain[0][:], w1_rounded[0])
+        for lo in (0, BANK):
+            nc.vector.tensor_copy(v_words[1][:, lo : lo + BANK], table1[:].indirect(entries(list1, lo, lo + BANK)))
+        w2w_reordered = held.tile([P, 2, H], U8, align_bytes=64)
         nc.vector.tensor_copy(
-            w2w_perm[:].bitcast(U16).rearrange("p a (t m) -> p a t m", t=PACK),
+            w2w_reordered[:].bitcast(U16).rearrange("p a (t m) -> p a t m", t=PACK),
             w2w[:, :, H:].bitcast(U16).rearrange("p a (m t) -> p a t m", t=PACK),
         )
 
-        def stationary(i, a):
-            if i < 4:
-                c1 = slice(P * a, P * (a + 1))
-                return (
-                    w1c_nat[i][:, c1].bitcast(FP8X4),
-                    w1s_nat[i][:, c1],
-                    w2w[:, a, 2 * P * i : 2 * P * (i + 1)].bitcast(FP4X4),
-                    w2s[:, a, P * i : P * (i + 1)],
-                )
-            t = i - 4
-            c1 = slice(P * t, P * (t + 1))
-            c2 = slice(K_PASS * a + P * t, K_PASS * a + P * (t + 1))
-            return (
-                codes["w1_codes"][:, c2].bitcast(FP8X4),
-                w1s_perm[:, c2],
-                w2w_perm[:, a, 2 * P * t : 2 * P * (t + 1)].bitcast(FP4X4),
-                w2s_perm[:, a, c1],
-            )
+        def w1_columns(i, a):
+            if i < PLAIN_TILES:
+                c = slice(P * a, P * (a + 1))
+                return w1c_plain[i][:, c].bitcast(FP8X4), w1s_plain[i][:, c]
+            first = K_PASS * a + P * (i - PLAIN_TILES)
+            c = slice(first, first + P)
+            return codes["w1_codes"][:, c].bitcast(FP8X4), w1s_reordered[:, c]
 
-        h = {}
-        x1 = {}
-        h_slots = [held.tile([P, S], F32, name="h%d" % u) for u in range(3)]
+        def w2_columns(i, a):
+            words, scales, u = (w2w, w2s, i) if i < PLAIN_TILES else (w2w_reordered, w2s_reordered, i - PLAIN_TILES)
+            return words[:, a, 2 * P * u : 2 * P * (u + 1)].bitcast(FP4X4), scales[:, a, P * u : P * (u + 1)]
 
-        def first_stage(i, half):
-            if half == 0:
-                h[i] = x1[5] if i == 7 else h_slots[i % 3]
-            c = slice(BANK * half, BANK * (half + 1))
+        first_read = {}
+        h_ring = [held.tile([P, S], F32, name="h%d" % u) for u in range(3)]
+
+        def h_tile(i):
+            return first_read[5] if i == LAST else h_ring[i % 3]
+
+        def larger_reading(i, lo, dst):
+            c = slice(lo, lo + BANK)
             h1 = psum.tile([P, BANK], F32, name="bank")
             h2 = psum.tile([P, BANK], F32, name="bank")
-            for acc, u in ((h1, 0), (h2, 2)):
+            for acc, columns in ((h1, w1_columns), (h2, w2_columns)):
                 for a in range(2):
-                    words, scales = stationary(i, a)[u : u + 2]
-                    moving = v_words[a][:, c].bitcast(FP8X4)
+                    words, scales = columns(i, a)
                     nc.tensor.matmul_mx(
-                        out=acc[:], lhsT=words, lhsT_scale=scales, rhs=moving, rhs_scale=v_scales[:, a, c],
-                        start=(a == 0), stop=(a == 1),
+                        out=acc[:], lhsT=words, lhsT_scale=scales, rhs=v_words[a][:, c].bitcast(FP8X4),
+                        rhs_scale=v_scales[:, a, c], start=(a == 0), stop=(a == 1),
                     )
             h1_sb = stage.tile([P, BANK], F32, name="h1_sb")
             nc.scalar.copy(h1_sb[:], h1[:])
-            if (i, half) == (0, 1):
-                second = chain.tile([P, BANK], F32, name="h0_second", align_bytes=64)
-                h["second"] = second[:]
-            nc.vector.tensor_tensor(h["second"] if (i, half) == (0, 1) else h[i][:, c], h2[:], h1_sb[:], MAX)
+            nc.vector.tensor_tensor(dst, h2[:], h1_sb[:], MAX)
 
-        def scatter(i, lo, hi):
-            weights = wgs_nat[:, lo:hi] if i < 4 else wgs_perm[:, i - 4, lo:hi]
-            nc.vector.tensor_tensor(page[i][:].indirect(cols(list2, lo, hi)), h["second"] if lo > 0 else h[i][:, lo:hi], weights, MULT)
+        def scatter(i, lo, hi, values):
+            weights = wgs_plain if i < PLAIN_TILES else wgs_rows[i - PLAIN_TILES]
+            nc.vector.tensor_tensor(page[i][:].indirect(entries(list2, lo, hi)), values, weights[:, lo:hi], MULT)
 
-        def fetch_first(i, lo, hi, dst):
-            nc.vector.tensor_copy(dst, page[i][:].indirect(cols(list3, lo, hi)))
-            return dst
+        def read_first(i, lo, hi, dst):
+            nc.vector.tensor_copy(dst, page[i][:].indirect(entries(list3, lo, hi)))
 
-        def first_tile(i, width):
-            if i in X_SLOT:
-                x = chain.tile([P, width], F32, name=X_SLOT[i], align_bytes=64)
-                return x[:]
-            x = work.tile([P, width], F32, name="x1")
-            return x[:]
+        def first_read_tile(i, width):
+            if i in FIRST_READ_BYTES:
+                return shared.tile([P, width], F32, name=FIRST_READ_BYTES[i], align_bytes=64)
+            return work.tile([P, width], F32, name="first_read")
 
-        def fetch_second(i, lo, hi, first):
-            if i == 5:
-                z = chain.tile([P, hi - lo], F32, name="z_rounded", align_bytes=64)
-            elif i == 1 or (i == 6 and lo == 0):
-                z = h[i + 1][:, 0 : hi - lo]
-            elif i < 5:
-                z = h[i][:, 0 : hi - lo]
-            else:
-                z = stage.tile([P, hi - lo], F32, name="z_tail")
-            nc.vector.tensor_tensor(z[:], page[i][:].indirect(cols(list4, lo, hi)), first, MULT)
-            if i < 4:
-                zb = work.tile([P, M], BF16, name="zb")
-                nc.scalar.activation(zb[:], z[:], COPY, scale=gain_nat[:, i : i + 1])
+        def read_second(i, lo, hi, first, z):
+            nc.vector.tensor_tensor(z, page[i][:].indirect(entries(list4, lo, hi)), first, MULT)
+            if i < PLAIN_TILES:
+                z_rows = work.tile([P, M], BF16, name="z_rows")
+                nc.scalar.activation(z_rows[:], z, COPY, scale=gain_plain[:, i : i + 1])
                 for t in range(PACK):
-                    nc.sync.dma_start(planes[32 * i : 32 * (i + 1), t, :], zb[t:P:PACK, :])
+                    nc.sync.dma_start(z_planes[32 * i : 32 * (i + 1), t, :], z_rows[t:P:PACK, :])
             else:
-                t = i - 4
-                for c_lo, c_hi in (CHUNK_A, CHUNK_B, CHUNK_C):
-                    a, b = max(lo, c_lo), min(hi, c_hi)
+                t = i - PLAIN_TILES
+                for part_lo, part_hi in (PART_A, PART_B, PART_C):
+                    a, b = max(lo, part_lo), min(hi, part_hi)
                     if a < b:
                         nc.scalar.activation(
-                            z_grouped[c_lo][:, a - c_lo : b - c_lo, t], z[:, a - lo : b - lo], COPY,
-                            scale=gain_perm[:, t : t + 1],
+                            z_words[part_lo][:, a - part_lo : b - part_lo, t], z[:, a - lo : b - lo], COPY,
+                            scale=gain_rows[:, t : t + 1],
                         )
 
-        first_stage(0, 0)
-        scatter(0, 0, BANK)
-        w1_grouped[1] = load_w1_natural(1)
+        larger_reading(0, 0, h_tile(0)[:, 0:BANK])
+        scatter(0, 0, BANK, h_tile(0)[:, 0:BANK])
+        w1_rounded[1] = load_w1_tile(1)
+        nc.sync.dma_start(wgs_plain[:, BANK:], wgs[:, BANK:])
         list3 = load_list("list3", offs3)
         list4 = load_list("list4", offs4)
-        w1_grouped[2] = load_w1_natural(2)
+        w1_rounded[2] = load_w1_tile(2)
         page[1] = load_page(1)
-        gain_nat = held.tile([P, 4], F32)
-        with nc.allow_non_contiguous_dma(reason="one value a partition"):
-            nc.sync.dma_start(gain_nat[:], gain[0:K_PASS].rearrange("(c p) -> p c", p=P))
-        quantize(w1c_nat[1][:], w1s_nat[1][:], w1_grouped[1])
-        first_stage(0, 1)
-        scatter(0, BANK, S)
-        x1[0] = fetch_first(0, 0, M, first_tile(0, M))
-        first_stage(1, 0)
-        first_stage(1, 1)
+        quantize(w1c_plain[1][:], w1s_plain[1][:], w1_rounded[1])
+        h0_second = shared.tile([P, BANK], F32, name="h0_second", align_bytes=64)
+        larger_reading(0, BANK, h0_second[:])
+        scatter(0, BANK, S, h0_second[:])
+        first_read[0] = first_read_tile(0, M)
+        read_first(0, 0, M, first_read[0][:])
+        for lo in (0, BANK):
+            larger_reading(1, lo, h_tile(1)[:, lo : lo + BANK])
 
-        planes = held.tile([P, PACK, M], BF16, align_bytes=64)
-        z_grouped = {
-            lo: chain.tile([P, hi - lo, PACK], BF16, name="z_late%d" % lo, align_bytes=64)
-            for lo, hi in (CHUNK_A, CHUNK_B, CHUNK_C)
+        z_planes = shared.tile([P, PACK, M], BF16, name="z_planes", align_bytes=64)
+        z_words = {
+            lo: shared.tile([P, hi - lo, PACK], BF16, name="z_words%d" % lo, align_bytes=64)
+            for lo, hi in (PART_A, PART_B, PART_C)
         }
-        wgs_perm = held.tile([P, PACK, S], F32)
-        gain_perm = held.tile([P, PACK], F32)
+        wgs_rows = [
+            shared.tile([P, S], F32, name="wgs%d" % t if t < PACK - 1 else "z_codes", align_bytes=64)
+            for t in range(PACK)
+        ]
+        gain_plain = held.tile([P, PLAIN_TILES], F32)
+        gain_rows = held.tile([P, PACK], F32)
         rel_sb = held.tile([P, N // P], F32)
 
-        for i in range(1, TILES - 1):
-            if i + 1 < 4:
-                quantize(w1c_nat[i + 1][:], w1s_nat[i + 1][:], w1_grouped[i + 1])
+        for i in range(1, LAST):
+            nxt = i + 1
+            if nxt < PLAIN_TILES:
+                quantize(w1c_plain[nxt][:], w1s_plain[nxt][:], w1_rounded[nxt])
             if i == 1:
-                w1_grouped[3] = load_w1_natural(3)
-                w1_perm = load_rows(w1[:, K_PASS:], True, "w1_rounded")
-            if i >= 3:
-                for q in range(4):
+                w1_rounded[3] = load_w1_tile(3)
+                w1_second_half = load_weight(w1[:, K_PASS:], "w1_rounded", True)
+                load_per_partition(gain_plain[:], gain[0:K_PASS])
+            if nxt >= PLAIN_TILES:
+                t = nxt - PLAIN_TILES
+                for q in range(QUADS):
                     nc.sync.dma_start(
-                        wgs_perm[32 * q : 32 * (q + 1), i - 3, :], wgs.rearrange("(p t) s -> t p s", t=PACK)[i - 3]
+                        wgs_rows[t][32 * q : 32 * (q + 1), :], wgs.rearrange("(p t) s -> t p s", t=PACK)[t]
                     )
-            if i == 3:
-                nc.sync.dma_start(gain_perm[:], gain[K_PASS:].rearrange("(p t) -> p t", t=PACK))
-            page[i + 1] = load_page(i + 1)
+            if nxt == PLAIN_TILES:
+                nc.sync.dma_start(gain_rows[:], gain[K_PASS:].rearrange("(p t) -> p t", t=PACK))
+            page[nxt] = load_page(nxt)
             if i == 2:
-                w3_grouped = load_rows(w3, False, "w3_rounded")
-            if i == 6:
-                with nc.allow_non_contiguous_dma(reason="one value a partition"):
-                    nc.sync.dma_start(rel_sb[:], rel.rearrange("(c p) -> p c", p=P))
-            scatter(i, 0, S)
-            if i < 6:
-                first_stage(i + 1, 0)
-            if i == 6:
-                grouped = chain.tile([P, M, PACK], BF16, name="z_rounded", align_bytes=64)
-                for half in range(2):
-                    c = slice(BANK * half, BANK * (half + 1))
-                    nc.scalar.copy(
-                        grouped[:, c, :].rearrange("p (c i) j -> p c j i", i=4),
-                        planes[:, :, c].rearrange("p j (c i) -> p c j i", i=4),
-                    )
-                quantize_into("z_codes", zs[0][:], grouped[:].rearrange("p c j -> p (c j)"))
-            fetch_second(i - 1, 0, M, x1[i - 1])
-            if i == 6:
-                first_stage(i + 1, 0)
-            first_stage(i + 1, 1)
-            width = M if i < 6 else BANK
-            x1[i] = fetch_first(i, 0, width, first_tile(i, width))
+                w3_rounded = load_weight(w3, "w3_rounded", False)
+            if nxt == LAST:
+                load_per_partition(rel_sb[:], rel)
+
+            scatter(i, 0, S, h_tile(i)[:])
+            if nxt < LAST:
+                larger_reading(nxt, 0, h_tile(nxt)[:, 0:BANK])
+                z = h_tile(2) if i == 2 else h_tile(i - 1)
+            else:
+                z_rounded = shared.tile([P, M, PACK], BF16, name="z_rounded", align_bytes=64)
+                for lo in (0, BANK):
+                    interleave(z_rounded[:, lo : lo + BANK, :], z_planes[:, :, lo : lo + BANK])
+                z = shared.tile([P, M], F32, name="z_planes", align_bytes=64)
+            read_second(i - 1, 0, M, first_read[i - 1][:], z[:])
+            if nxt == LAST:
+                larger_reading(nxt, 0, h_tile(nxt)[:, 0:BANK])
+            larger_reading(nxt, BANK, h_tile(nxt)[:, BANK:])
+            width = M if nxt < LAST else PART_A[1]
+            first_read[i] = first_read_tile(i, width)
+            read_first(i, 0, width, first_read[i][:])
             if i == 2:
-                quantize_into("w1_codes", w1s_perm[:], w1_perm)
+                quantize_shared("w1_codes", w1s_reordered[:], w1_second_half)
             if i == 4:
-                quantize_into("w3_codes", w3s[:], w3_grouped)
+                quantize_shared("w3_codes", w3s[:], w3_rounded)
 
         staged = big.tile([P, N // P, M], F32, name="big", align_bytes=64)
         out_view = out.rearrange("(i p) m -> p i m", p=P)
-        zc = [codes["z_codes"], zc_late]
 
-        def last_product(lo, hi, base):
+        def last_product(lo, hi, part_lo):
             width = hi - lo
             per_bank = 1 if width == BANK else 2
-            rounded = z_grouped[base][:, lo - base : hi - base, :]
-            quantize(zc[1][:, lo:hi], zs[1][:, lo:hi], rounded.rearrange("p c j -> p (c j)"))
+            rounded = z_words[part_lo][:, lo - part_lo : hi - part_lo, :]
+            quantize(z_codes1[:, lo:hi], zs[1][:, lo:hi], rounded.rearrange("p c j -> p (c j)"))
             for g in range(N // P // per_bank):
                 acc = psum.tile([P, per_bank, width], F32, name="bank")
-                for b in range(2):
+                for b, z_codes in enumerate((codes["z_codes"], z_codes1)):
                     for u in range(per_bank):
                         first = N * b + P * (g * per_bank + u)
                         n = slice(first, first + P)
                         nc.tensor.matmul_mx(
                             out=acc[:, u, :], lhsT=codes["w3_codes"][:, n].bitcast(FP8X4), lhsT_scale=w3s[:, n],
-                            rhs=zc[b][:, lo:hi].bitcast(FP8X4), rhs_scale=zs[b][:, lo:hi],
+                            rhs=z_codes[:, lo:hi].bitcast(FP8X4), rhs_scale=zs[b][:, lo:hi],
                             start=(b == 0 and u == 0), stop=(b == 1 and u == per_bank - 1),
                         )
                 for u in range(per_bank):
-                    i = g * per_bank + u
-                    if i >= 2:
-                        nc.vector.tensor_scalar_mul(staged[:, i, lo:hi], acc[:, u, :], rel_sb[:, i : i + 1])
+                    tile = g * per_bank + u
+                    factor = rel_sb[:, tile : tile + 1]
+                    if tile < 2:
+                        nc.scalar.activation(staged[:, tile, lo:hi], acc[:, u, :], COPY, scale=factor)
                     else:
-                        nc.scalar.activation(staged[:, i, lo:hi], acc[:, u, :], COPY, scale=rel_sb[:, i : i + 1])
-                rows = slice(g * per_bank, (g + 1) * per_bank)
-                nc.sync.dma_start(out_view[:, rows, lo:hi], staged[:, rows, lo:hi])
+                        nc.vector.tensor_scalar_mul(staged[:, tile, lo:hi], acc[:, u, :], factor)
+                tiles = slice(g * per_bank, (g + 1) * per_bank)
+                nc.sync.dma_start(out_view[:, tiles, lo:hi], staged[:, tiles, lo:hi])
 
-        scatter(7, 0, S)
-        x6 = chain.tile([P, CHUNK_B[1] - CHUNK_B[0]], F32, name="z_rounded", align_bytes=64)
-        fetch_first(6, *CHUNK_B, x6[:])
-        fetch_second(6, *CHUNK_A, x1[6])
-        x7 = first_tile(7, CHUNK_B[1])
-        fetch_first(7, *CHUNK_A, x7[:, 0:BANK])
-        fetch_second(6, *CHUNK_B, x6[:])
-        fetch_second(7, *CHUNK_A, x7[:, 0:BANK])
-        fetch_first(7, *CHUNK_B, x7[:, BANK:])
-        x_last = chain.tile([P, 2, CHUNK_C[1] - CHUNK_C[0]], F32, name="w3_rounded", align_bytes=64)
-        fetch_first(7, *CHUNK_C, x_last[:, 1, :])
-        fetch_second(7, *CHUNK_B, x7[:, BANK:])
-        last_product(*CHUNK_A, CHUNK_A[0])
-        x6_last = chain.tile([P, CHUNK_C[1] - CHUNK_C[0]], F32, name="z_late0", align_bytes=64)
-        fetch_first(6, *CHUNK_C, x6_last[:])
-        fetch_second(7, 768, 896, x_last[:, 1, 0:P])
-        fetch_second(6, *CHUNK_C, x6_last[:])
-        last_product(*CHUNK_B, CHUNK_B[0])
-        fetch_second(7, 896, 1024, x_last[:, 1, P:])
-        last_product(768, 896, CHUNK_C[0])
-        last_product(896, 1024, CHUNK_C[0])
+        def read_second_part(i, part, first):
+            z_part = stage.tile([P, part[1] - part[0]], F32, name="z_part")
+            read_second(i, *part, first, z_part[:])
+
+        def part_tile(part, name):
+            return shared.tile([P, part[1] - part[0]], F32, name=name, align_bytes=64)
+
+        before = LAST - 1
+        scatter(LAST, 0, S, h_tile(LAST)[:])
+        before_b = part_tile(PART_B, "z_planes")
+        read_first(before, *PART_B, before_b[:])
+        read_second(before, *PART_A, first_read[before][:], h_tile(LAST)[:, 0:BANK])
+        last_ab = first_read_tile(LAST, PART_B[1])
+        read_first(LAST, *PART_A, last_ab[:, 0:BANK])
+        quantize_shared("z_codes", zs[0][:], z_rounded[:].rearrange("p c j -> p (c j)"))
+        read_second_part(before, PART_B, before_b[:])
+        read_second_part(LAST, PART_A, last_ab[:, 0:BANK])
+        read_first(LAST, *PART_B, last_ab[:, BANK:])
+        last_c = part_tile(PART_C, "w3_rounded")
+        read_first(LAST, *PART_C, last_c[:])
+        read_second_part(LAST, PART_B, last_ab[:, BANK:])
+        last_product(*PART_A, PART_A[0])
+        before_c = part_tile(PART_C, "z_words0")
+        read_first(before, *PART_C, before_c[:])
+        read_second_part(LAST, PART_C1, last_c[:, 0:P])
+        read_second_part(before, PART_C, before_c[:])
+        last_product(*PART_B, PART_B[0])
+        read_second_part(LAST, PART_C2, last_c[:, P:])
+        last_product(*PART_C1, PART_C[0])
+        last_product(*PART_C2, PART_C[0])

from contextlib import ExitStack

import concourse.mybir as mybir

K, H, N, T, S, T2, M = 1024, 1024, 512, 4096, 1024, 2048, 1024
FLOPS = 2 * (2 * K * H * S + H * N * M)

F32 = mybir.dt.float32
BF16 = mybir.dt.bfloat16
I32 = mybir.dt.int32
U32 = mybir.dt.uint32
U16 = mybir.dt.uint16
U8 = mybir.dt.uint8
FP8X4 = mybir.dt.float8_e4m3fn_x4
FP4X4 = mybir.dt.float4_e2m1fn_x4
MULT = mybir.AluOpType.mult
MAX = mybir.AluOpType.max
COPY = mybir.ActivationFunctionType.Copy

P = 128
PACK = 4
K_PASS = P * PACK
BANK = 512
QUADS = 4
PLAIN_TILES = 4
LAST = H // P - 1
RUN = 4

PART_A, PART_B, PART_C = (0, 512), (512, 768), (768, 1024)
PART_C1, PART_C2 = (768, 896), (896, 1024)

W1_STAGING = ("z_words0", "x5", "z_codes", "z_rounded")
FIRST_READ_BYTES = {1: "w1_codes", 3: "w3_codes", 5: "x5"}


def tile_list_royal_succession_features_kernel(
    tc, tab_words, tab_scales, offs, w1, w2_words, w2_scales, page0, wgs, offs2, offs3, offs4, gain, w3, rel, out
):
    nc = tc.nc
    with ExitStack() as ctx:
        held = ctx.enter_context(tc.tile_pool(name="held", bufs=1))
        big = ctx.enter_context(tc.tile_pool(name="big", bufs=2))
        pages = ctx.enter_context(tc.tile_pool(name="pages", bufs=5))
        stage = ctx.enter_context(tc.tile_pool(name="stage", bufs=3))
        work = ctx.enter_context(tc.tile_pool(name="work", bufs=2))
        shared = ctx.enter_context(tc.tile_pool(name="shared", bufs=1))
        psum = ctx.enter_context(tc.psum_pool(name="psum", bufs=8))

        def load_list(name, src):
            lst = held.tile([P, S // 16], U16, name=name)
            nc.sync.dma_start(lst[:], src)
            return lst

        def entries(lst, lo, hi):
            return lst[:, lo // 16 : hi // 16]

        def load_table(a):
            words = big.tile([P, T], U32, name="big", align_bytes=64)
            nc.sync.dma_start(words[:].bitcast(I32), tab_words[a].rearrange("p t i -> p (t i)").bitcast(I32))
            return words

        def interleave(dst, src):
            nc.scalar.copy(dst.rearrange("p (c i) j -> p c j i", i=RUN), src.rearrange("p j (c i) -> p c j i", i=RUN))

        def load_w1_tile(i):
            raw = shared.tile([P, 2, PACK, P], F32, name=W1_STAGING[i], align_bytes=64)
            for a in range(2):
                rows = w1[K_PASS * a : K_PASS * (a + 1), P * i : P * (i + 1)]
                nc.sync.dma_start(raw[:, a, :, :], rows.rearrange("(p j) c -> p j c", j=PACK))
            if i == 1:
                rounded = shared.tile([P, 2, P, PACK], BF16, name="h0_second", align_bytes=64)
            else:
                rounded = stage.tile([P, 2, P, PACK], BF16, name="w1_rounded_tile", align_bytes=64)
            for a in range(2):
                interleave(rounded[:, a, :, :], raw[:, a, :, :])
            return rounded[:].rearrange("p a c j -> p (a c j)")

        def load_weight(src, name, reorder_columns):
            rounded = shared.tile([P, 2, BANK, PACK], BF16, name=name, align_bytes=64)
            raw = big.tile([P, 2, PACK, BANK], F32, name="big", align_bytes=64)
            for a in range(2):
                rows = src[K_PASS * a : K_PASS * (a + 1), :]
                nc.sync.dma_start(raw[:, a, :, :], rows.rearrange("(p j) c -> p j c", j=PACK))
                if reorder_columns:
                    nc.scalar.copy(
                        rounded[:, a, :, :].rearrange("p (t m) j -> p m t j", t=PACK),
                        raw[:, a, :, :].rearrange("p j (m t) -> p m t j", t=PACK),
                    )
                else:
                    interleave(rounded[:, a, :, :], raw[:, a, :, :])
            return rounded[:].rearrange("p a c j -> p (a c j)")

        def load_page(i):
            tile = pages.tile([P, T2], F32, name="page")
            if i < PLAIN_TILES:
                rows = page0[P * i : P * (i + 1), :]
            else:
                rows = page0[K_PASS:, :].rearrange("(p t) c -> t p c", t=PACK)[i - PLAIN_TILES]
            nc.sync.dma_start(tile[:], rows)
            return tile

        def load_per_partition(dst, src):
            with nc.allow_non_contiguous_dma(reason="one value a partition"):
                nc.sync.dma_start(dst, src.rearrange("(c p) -> p c", p=P))

        def quantize(words, scales, rounded):
            nc.vector.quantize_mx(out=words.bitcast(FP8X4), scales=scales, in_=rounded)

        codes = {}

        def quantize_shared(name, scales, rounded):
            codes[name] = shared.tile([P, M], U32, name=name, align_bytes=64)
            quantize(codes[name][:], scales, rounded)

        scale_rows = held.tile([P, T], U8, align_bytes=64)
        nc.vector.memset(scale_rows[32:64, :].bitcast(I32), 0)
        nc.vector.memset(scale_rows[64:128, :].bitcast(I32), 0)
        w2s = held.tile([P, 2, H], U8, align_bytes=64)
        nc.gpsimd.memset(w2s[:].rearrange("p a c -> p (a c)").bitcast(I32), 0)
        v_scales = held.tile([P, 2, S], U8, align_bytes=64)
        nc.vector.memset(v_scales[:].rearrange("p a c -> p (a c)").bitcast(I32), 0)
        for q in range(QUADS):
            nc.gpsimd.dma_start(
                w2s[32 * q : 32 * q + 4, :, :].bitcast(I32),
                w2_scales[:, 4 * q : 4 * q + 4, :].rearrange("a r c -> r a c").bitcast(I32),
            )

        list1 = load_list("list1", offs)
        nc.sync.dma_start(scale_rows[0:32, :].bitcast(I32), tab_scales.rearrange("a q t -> q a t").bitcast(I32))
        table0 = load_table(0)
        w1_rounded = {0: load_w1_tile(0)}
        list2 = load_list("list2", offs2)
        table1 = load_table(1)
        w2w = held.tile([P, 2, 2 * H], U8, align_bytes=64)
        nc.sync.dma_start(w2w[:].bitcast(I32), w2_words.rearrange("a p c -> p a c").bitcast(I32))
        wgs_plain = held.tile([P, S], F32)
        nc.sync.dma_start(wgs_plain[:, 0:BANK], wgs[:, 0:BANK])
        page = {0: load_page(0)}

        picked_scales = held.tile([P, S], U8, align_bytes=64)
        nc.vector.tensor_copy(picked_scales[:], scale_rows[:].indirect(list1[:]))
        for q in range(QUADS):
            nc.scalar.dma_start(
                v_scales[32 * q : 32 * q + 4, :, :].bitcast(I32), picked_scales[8 * q : 8 * q + 8, :].bitcast(I32)
            )
        v_words = [held.tile([P, S], U32, name="v_words%d" % a, align_bytes=64) for a in range(2)]
        nc.vector.tensor_copy(v_words[0][:], table0[:].indirect(list1[:]))

        w2s_reordered = held.tile([P, 2, K_PASS], U8, align_bytes=64)
        nc.vector.tensor_copy(
            w2s_reordered[:].rearrange("p a (t m) -> p a t m", t=PACK),
            w2s[:, :, K_PASS:].rearrange("p a (m t) -> p a t m", t=PACK),
        )

        w1c_plain = [held.tile([P, 2 * P], U32, name="w1c%d" % i, align_bytes=64) for i in range(PLAIN_TILES)]
        w1s_plain = [held.tile([P, 2 * P], U8, name="w1s%d" % i, align_bytes=64) for i in range(PLAIN_TILES)]
        w1s_reordered = held.tile([P, 2 * K_PASS], U8, align_bytes=64)
        w3s = held.tile([P, 2 * N], U8, align_bytes=64)
        zs = [held.tile([P, M], U8, name="zs%d" % b, align_bytes=64) for b in range(2)]
        z_codes1 = held.tile([P, M], U32, align_bytes=64)

        quantize(w1c_plain[0][:], w1s_plain[0][:], w1_rounded[0])
        for lo in (0, BANK):
            nc.vector.tensor_copy(v_words[1][:, lo : lo + BANK], table1[:].indirect(entries(list1, lo, lo + BANK)))
        w2w_reordered = held.tile([P, 2, H], U8, align_bytes=64)
        nc.vector.tensor_copy(
            w2w_reordered[:].bitcast(U16).rearrange("p a (t m) -> p a t m", t=PACK),
            w2w[:, :, H:].bitcast(U16).rearrange("p a (m t) -> p a t m", t=PACK),
        )

        def w1_columns(i, a):
            if i < PLAIN_TILES:
                c = slice(P * a, P * (a + 1))
                return w1c_plain[i][:, c].bitcast(FP8X4), w1s_plain[i][:, c]
            first = K_PASS * a + P * (i - PLAIN_TILES)
            c = slice(first, first + P)
            return codes["w1_codes"][:, c].bitcast(FP8X4), w1s_reordered[:, c]

        def w2_columns(i, a):
            words, scales, u = (w2w, w2s, i) if i < PLAIN_TILES else (w2w_reordered, w2s_reordered, i - PLAIN_TILES)
            return words[:, a, 2 * P * u : 2 * P * (u + 1)].bitcast(FP4X4), scales[:, a, P * u : P * (u + 1)]

        first_read = {}
        h_ring = [held.tile([P, S], F32, name="h%d" % u) for u in range(3)]

        def h_tile(i):
            return first_read[5] if i == LAST else h_ring[i % 3]

        def larger_reading(i, lo, dst):
            c = slice(lo, lo + BANK)
            h1 = psum.tile([P, BANK], F32, name="bank")
            h2 = psum.tile([P, BANK], F32, name="bank")
            for acc, columns in ((h1, w1_columns), (h2, w2_columns)):
                for a in range(2):
                    words, scales = columns(i, a)
                    nc.tensor.matmul_mx(
                        out=acc[:], lhsT=words, lhsT_scale=scales, rhs=v_words[a][:, c].bitcast(FP8X4),
                        rhs_scale=v_scales[:, a, c], start=(a == 0), stop=(a == 1),
                    )
            h1_sb = stage.tile([P, BANK], F32, name="h1_sb")
            nc.scalar.copy(h1_sb[:], h1[:])
            nc.vector.tensor_tensor(dst, h2[:], h1_sb[:], MAX)

        def scatter(i, lo, hi, values):
            weights = wgs_plain if i < PLAIN_TILES else wgs_rows[i - PLAIN_TILES]
            nc.vector.tensor_tensor(page[i][:].indirect(entries(list2, lo, hi)), values, weights[:, lo:hi], MULT)

        def read_first(i, lo, hi, dst):
            nc.vector.tensor_copy(dst, page[i][:].indirect(entries(list3, lo, hi)))

        def first_read_tile(i, width):
            if i in FIRST_READ_BYTES:
                return shared.tile([P, width], F32, name=FIRST_READ_BYTES[i], align_bytes=64)
            return work.tile([P, width], F32, name="first_read")

        def read_second(i, lo, hi, first, z):
            nc.vector.tensor_tensor(z, page[i][:].indirect(entries(list4, lo, hi)), first, MULT)
            if i < PLAIN_TILES:
                z_rows = work.tile([P, M], BF16, name="z_rows")
                nc.scalar.activation(z_rows[:], z, COPY, scale=gain_plain[:, i : i + 1])
                for t in range(PACK):
                    nc.sync.dma_start(z_planes[32 * i : 32 * (i + 1), t, :], z_rows[t:P:PACK, :])
            else:
                t = i - PLAIN_TILES
                for part_lo, part_hi in (PART_A, PART_B, PART_C):
                    a, b = max(lo, part_lo), min(hi, part_hi)
                    if a < b:
                        nc.scalar.activation(
                            z_words[part_lo][:, a - part_lo : b - part_lo, t], z[:, a - lo : b - lo], COPY,
                            scale=gain_rows[:, t : t + 1],
                        )

        larger_reading(0, 0, h_tile(0)[:, 0:BANK])
        scatter(0, 0, BANK, h_tile(0)[:, 0:BANK])
        w1_rounded[1] = load_w1_tile(1)
        nc.sync.dma_start(wgs_plain[:, BANK:], wgs[:, BANK:])
        list3 = load_list("list3", offs3)
        list4 = load_list("list4", offs4)
        w1_rounded[2] = load_w1_tile(2)
        page[1] = load_page(1)
        quantize(w1c_plain[1][:], w1s_plain[1][:], w1_rounded[1])
        h0_second = shared.tile([P, BANK], F32, name="h0_second", align_bytes=64)
        larger_reading(0, BANK, h0_second[:])
        scatter(0, BANK, S, h0_second[:])
        first_read[0] = first_read_tile(0, M)
        read_first(0, 0, M, first_read[0][:])
        for lo in (0, BANK):
            larger_reading(1, lo, h_tile(1)[:, lo : lo + BANK])

        z_planes = shared.tile([P, PACK, M], BF16, name="z_planes", align_bytes=64)
        z_words = {
            lo: shared.tile([P, hi - lo, PACK], BF16, name="z_words%d" % lo, align_bytes=64)
            for lo, hi in (PART_A, PART_B, PART_C)
        }
        wgs_rows = [
            shared.tile([P, S], F32, name="wgs%d" % t if t < PACK - 1 else "z_codes", align_bytes=64)
            for t in range(PACK)
        ]
        gain_plain = held.tile([P, PLAIN_TILES], F32)
        gain_rows = held.tile([P, PACK], F32)
        rel_sb = held.tile([P, N // P], F32)

        for i in range(1, LAST):
            nxt = i + 1
            if nxt < PLAIN_TILES:
                quantize(w1c_plain[nxt][:], w1s_plain[nxt][:], w1_rounded[nxt])
            if i == 1:
                w1_rounded[3] = load_w1_tile(3)
                w1_second_half = load_weight(w1[:, K_PASS:], "w1_rounded", True)
                load_per_partition(gain_plain[:], gain[0:K_PASS])
            if nxt >= PLAIN_TILES:
                t = nxt - PLAIN_TILES
                for q in range(QUADS):
                    nc.sync.dma_start(
                        wgs_rows[t][32 * q : 32 * (q + 1), :], wgs.rearrange("(p t) s -> t p s", t=PACK)[t]
                    )
            if nxt == PLAIN_TILES:
                nc.sync.dma_start(gain_rows[:], gain[K_PASS:].rearrange("(p t) -> p t", t=PACK))
            page[nxt] = load_page(nxt)
            if i == 2:
                w3_rounded = load_weight(w3, "w3_rounded", False)
            if nxt == LAST:
                load_per_partition(rel_sb[:], rel)

            scatter(i, 0, S, h_tile(i)[:])
            if nxt < LAST:
                larger_reading(nxt, 0, h_tile(nxt)[:, 0:BANK])
                z = h_tile(2) if i == 2 else h_tile(i - 1)
            else:
                z_rounded = shared.tile([P, M, PACK], BF16, name="z_rounded", align_bytes=64)
                for lo in (0, BANK):
                    interleave(z_rounded[:, lo : lo + BANK, :], z_planes[:, :, lo : lo + BANK])
                z = shared.tile([P, M], F32, name="z_planes", align_bytes=64)
            read_second(i - 1, 0, M, first_read[i - 1][:], z[:])
            if nxt == LAST:
                larger_reading(nxt, 0, h_tile(nxt)[:, 0:BANK])
            larger_reading(nxt, BANK, h_tile(nxt)[:, BANK:])
            width = M if nxt < LAST else PART_A[1]
            first_read[i] = first_read_tile(i, width)
            read_first(i, 0, width, first_read[i][:])
            if i == 2:
                quantize_shared("w1_codes", w1s_reordered[:], w1_second_half)
            if i == 4:
                quantize_shared("w3_codes", w3s[:], w3_rounded)

        staged = big.tile([P, N // P, M], F32, name="big", align_bytes=64)
        out_view = out.rearrange("(i p) m -> p i m", p=P)

        def last_product(lo, hi, part_lo):
            width = hi - lo
            per_bank = 1 if width == BANK else 2
            rounded = z_words[part_lo][:, lo - part_lo : hi - part_lo, :]
            quantize(z_codes1[:, lo:hi], zs[1][:, lo:hi], rounded.rearrange("p c j -> p (c j)"))
            for g in range(N // P // per_bank):
                acc = psum.tile([P, per_bank, width], F32, name="bank")
                for b, z_codes in enumerate((codes["z_codes"], z_codes1)):
                    for u in range(per_bank):
                        first = N * b + P * (g * per_bank + u)
                        n = slice(first, first + P)
                        nc.tensor.matmul_mx(
                            out=acc[:, u, :], lhsT=codes["w3_codes"][:, n].bitcast(FP8X4), lhsT_scale=w3s[:, n],
                            rhs=z_codes[:, lo:hi].bitcast(FP8X4), rhs_scale=zs[b][:, lo:hi],
                            start=(b == 0 and u == 0), stop=(b == 1 and u == per_bank - 1),
                        )
                for u in range(per_bank):
                    tile = g * per_bank + u
                    factor = rel_sb[:, tile : tile + 1]
                    if tile < 2:
                        nc.scalar.activation(staged[:, tile, lo:hi], acc[:, u, :], COPY, scale=factor)
                    else:
                        nc.vector.tensor_scalar_mul(staged[:, tile, lo:hi], acc[:, u, :], factor)
                tiles = slice(g * per_bank, (g + 1) * per_bank)
                nc.sync.dma_start(out_view[:, tiles, lo:hi], staged[:, tiles, lo:hi])

        def read_second_part(i, part, first):
            z_part = stage.tile([P, part[1] - part[0]], F32, name="z_part")
            read_second(i, *part, first, z_part[:])

        def part_tile(part, name):
            return shared.tile([P, part[1] - part[0]], F32, name=name, align_bytes=64)

        before = LAST - 1
        scatter(LAST, 0, S, h_tile(LAST)[:])
        before_b = part_tile(PART_B, "z_planes")
        read_first(before, *PART_B, before_b[:])
        read_second(before, *PART_A, first_read[before][:], h_tile(LAST)[:, 0:BANK])
        last_ab = first_read_tile(LAST, PART_B[1])
        read_first(LAST, *PART_A, last_ab[:, 0:BANK])
        quantize_shared("z_codes", zs[0][:], z_rounded[:].rearrange("p c j -> p (c j)"))
        read_second_part(before, PART_B, before_b[:])
        read_second_part(LAST, PART_A, last_ab[:, 0:BANK])
        read_first(LAST, *PART_B, last_ab[:, BANK:])
        last_c = part_tile(PART_C, "w3_rounded")
        read_first(LAST, *PART_C, last_c[:])
        read_second_part(LAST, PART_B, last_ab[:, BANK:])
        last_product(*PART_A, PART_A[0])
        before_c = part_tile(PART_C, "z_words0")
        read_first(before, *PART_C, before_c[:])
        read_second_part(LAST, PART_C1, last_c[:, 0:P])
        read_second_part(before, PART_C, before_c[:])
        last_product(*PART_B, PART_B[0])
        read_second_part(LAST, PART_C2, last_c[:, P:])
        last_product(*PART_C1, PART_C[0])
        last_product(*PART_C2, PART_C[0])
